import numpy as np
import ml_dtypes


def mxq(x, axis, fmt="e4m3"):
    dtype, down = {"e4m3": (ml_dtypes.float8_e4m3fn, 7), "e5m2": (ml_dtypes.float8_e5m2, 14)}[fmt]
    v = np.moveaxis(np.asarray(x, np.float32).astype(ml_dtypes.bfloat16).astype(np.float64), axis, -1)
    blocks = v.reshape(v.shape[:-1] + (-1, 32))
    amax = np.abs(blocks).max(-1, keepdims=True)
    byte = np.maximum(np.where(amax > 0, np.frexp(amax)[1] - 1 + 127, 0) - down, 1)
    scale = np.exp2(byte - 127.0)
    codes = (blocks / scale).astype(np.float32).astype(dtype).astype(np.float64)
    return np.moveaxis((codes * scale).reshape(v.shape), -1, axis)


WIDE = False


def mx_kscale(k):
    if not WIDE:
        return np.ones(k)
    levels = np.array([10, -10, 5, -5, 0])
    if k % 512:
        return np.exp2(np.random.permutation(np.resize(levels, k // 32))).repeat(32)
    a = np.empty((k // 512, 16))
    for p in range(k // 512):
        a[p, :8] = np.random.permutation(np.resize(levels, 8))
        for g in range(8):
            far = levels[np.abs(levels - a[p, g]) >= 10]
            a[p, g + 8] = far[np.random.randint(len(far))]
    return np.exp2(a.ravel()).repeat(32)


def f64(x):
    return np.asarray(x).astype(np.float64)


def striped(idx):
    return np.tile(idx.reshape(-1, 16).T, (8, 1)).astype(np.uint16)


def unstriped(offs):
    return offs[:16].T.reshape(-1).astype(np.int64)


E2M1 = np.array([0.0, 0.5, 1.0, 1.5, 2.0, 3.0, 4.0, 6.0, -0.0, -0.5, -1.0, -1.5, -2.0, -3.0, -4.0, -6.0])


def pack_weight(w, fmt):
    k, n = w.shape
    w = f64(np.asarray(w, np.float32).astype(ml_dtypes.bfloat16)).reshape(k // 32, 32, n)
    amax = np.abs(w).max(1)
    if fmt == "e4m3":
        byte = np.frexp(amax)[1] - 1 + 127 - 7
    else:
        mant, ex = np.frexp(amax / 6.0)
        byte = np.where(mant > 0.5, ex, ex - 1) + 127
    byte = np.clip(np.where(amax > 0, byte, 1), 1, 254)
    scaled = (w * np.exp2(127.0 - byte)[:, None, :]).reshape(k, n).astype(np.float32)
    by_word = np.ascontiguousarray(scaled.reshape(k // 512, 128, 4, n).transpose(0, 1, 3, 2))
    if fmt == "e4m3":
        words = by_word.astype(ml_dtypes.float8_e4m3fn).view(np.uint8)
    else:
        c = by_word.astype(ml_dtypes.float4_e2m1fn).view(np.uint8) & 0xF
        words = (c[..., 0::2] | (c[..., 1::2] << 4)).reshape(k // 512, 128, 2 * n)
    return np.ascontiguousarray(words), np.ascontiguousarray(byte.astype(np.uint8).reshape(k // 512, 16, n))


def unpack_weight(words, scales, fmt):
    g, _, n = scales.shape
    words = np.ascontiguousarray(words).reshape(g, 128, n, -1)
    if fmt == "e4m3":
        vals = words.view(ml_dtypes.float8_e4m3fn).astype(np.float64)
    else:
        nib = np.empty((g, 128, n, 4), np.uint8)
        nib[..., 0::2] = words & 0xF
        nib[..., 1::2] = words >> 4
        vals = E2M1[nib]
    vals = vals * np.repeat(np.exp2(scales.astype(np.float64) - 127.0), 8, axis=1)[..., None]
    return vals.transpose(0, 1, 3, 2).reshape(g * 512, n)


def gelu(v):
    return 0.5 * v * (1.0 + np.tanh(np.sqrt(2.0 / np.pi) * (v + 0.044715 * v**3)))


K, KX, KE, H, T, S, T2, S2 = 1536, 1024, 512, 1024, 2048, 1024, 1024, 512

def setup_inputs():
    n = np.random.standard_normal
    s = mx_kscale(K)[:, None]
    u = mx_kscale(H)[:, None]
    tab_words, tab_scales = pack_weight(n((K, T)) * s, "e4m3")
    tab2_words, tab2_scales = pack_weight(n((H, T2)) / np.sqrt(H) / u, "e4m3")
    w4_words, w4_scales = pack_weight(n((KE, H)) / np.sqrt(K) / s[KX:] * u.T, "e2m1")
    return {
        "tab_words": tab_words, "tab_scales": tab_scales,
        "offs": striped(np.random.permutation(T)[:S]),
        "tab2_words": tab2_words, "tab2_scales": tab2_scales,
        "offs2": striped(np.random.permutation(T2)[:S2]),
        "w1": (n((KX, H)) / np.sqrt(K) / s[:KX] * u.T).astype(np.float32),
        "w4_words": w4_words, "w4_scales": w4_scales,
        "lo": (-np.exp(0.3 * n(H)) * u[:, 0]).astype(np.float32),
        "hi": (np.exp(0.3 * n(H)) * u[:, 0]).astype(np.float32),
        "gain": np.exp(0.3 * n(S)).astype(np.float32),
        "cmin": (-0.8 * np.exp(0.3 * n(S2))).astype(np.float32),
        "cmax": (0.8 * np.exp(0.3 * n(S2))).astype(np.float32),
    }

def reference(tab_words, tab_scales, offs, tab2_words, tab2_scales, offs2, w1, w4_words, w4_scales, lo, hi, gain, cmin, cmax):
    v = unpack_weight(tab_words, tab_scales, "e4m3")[:, unstriped(offs)]
    v2 = unpack_weight(tab2_words, tab2_scales, "e4m3")[:, unstriped(offs2)]
    w4 = unpack_weight(w4_words, w4_scales, "e2m1")
    p = mxq(f64(w1), 0, "e4m3").T @ v[:KX] + w4.T @ v[KX:]
    h = np.minimum(np.maximum(p, f64(lo)[:, None]), f64(hi)[:, None])
    y = v2.T @ mxq(h, 0, "e4m3")
    c = y * f64(gain)[None, :]
    return np.minimum(np.maximum(c, f64(cmin)[:, None]), f64(cmax)[:, None])

@@ -1,0 +1,227 @@
+from contextlib import ExitStack
+
+import concourse.mybir as mybir
+
+F32 = mybir.dt.float32
+BF16 = mybir.dt.bfloat16
+I32 = mybir.dt.int32
+U32 = mybir.dt.uint32
+U16 = mybir.dt.uint16
+U8 = mybir.dt.uint8
+FP8X4 = mybir.dt.float8_e4m3fn_x4
+FP4X4 = mybir.dt.float4_e2m1fn_x4
+ALU = mybir.AluOpType
+
+P = 128
+K, KX, KE, H, T, S, T2, S2 = 1536, 1024, 512, 1024, 2048, 1024, 1024, 512
+N = 512
+FLOPS = 2 * K * H * S + 2 * H * S2 * S
+
+
+def tile_list_clamped_actuator_commands_kernel(
+    tc, tab_words, tab_scales, offs, tab2_words, tab2_scales, offs2, w1, w4_words, w4_scales, lo, hi, gain, cmin, cmax, out
+):
+    nc = tc.nc
+    with ExitStack() as ctx:
+        keep = ctx.enter_context(tc.tile_pool(name="keep", bufs=1))
+        psum = ctx.enter_context(tc.psum_pool(name="psum", bufs=8))
+
+        def held(shape, dtype, name):
+            return keep.tile(shape, dtype, name=name, align_bytes=64)
+
+        offs_sb = keep.tile([P, S // 16], U16, name="offs_sb")
+        offs2_sb = keep.tile([P, S2 // 16], U16, name="offs2_sb")
+        tab_w = [held([P, T], I32, "tab_w%d" % a) for a in range(3)]
+        tab_s = held([P, T // 4], I32, "tab_s")
+        tab2_w = held([P, 2, T2], I32, "tab2_w")
+        tab2_s = held([P, T2 // 4], I32, "tab2_s")
+        w4_raw = held([P, H // 2], I32, "w4_raw")
+        w4s_raw = held([P, H // 4], I32, "w4s_raw")
+        w1_raw = {(a, b): held([P, 4, N], F32, "w1_raw%d%d" % (a, b)) for a in range(2) for b in range(2)}
+        lo_sb = held([P, 2, 4], F32, "lo_sb")
+        hi_sb = held([P, 2, 4], F32, "hi_sb")
+        cmin_sb = held([P, 4], F32, "cmin_sb")
+        cmax_sb = held([P, 4], F32, "cmax_sb")
+        gain_sb = held([P, S], F32, "gain_sb")
+
+        nc.vector.memset(w4s_raw[:], 0)
+        nc.vector.memset(tab_s[:], 0)
+        nc.vector.memset(tab2_s[:], 0)
+
+        def load_tab(a):
+            nc.sync.dma_start(tab_w[a][:], tab_words[a].rearrange("p t i -> p (t i)").bitcast(I32))
+
+        def load_w1(a, b):
+            rows = w1[512 * a : 512 * (a + 1), N * b : N * (b + 1)]
+            nc.sync.dma_start(w1_raw[a, b][:], rows.rearrange("(p j) c -> p j c", j=4))
+
+        tab_s32 = tab_scales.bitcast(I32)
+        tab2_s32 = tab2_scales.bitcast(I32)
+        w4_s32 = w4_scales.bitcast(I32)
+
+        for r in range(4):
+            nc.gpsimd.dma_start(w4s_raw[r:P:32, :], w4_s32[0, r:16:4, :])
+        with nc.allow_non_contiguous_dma(reason="short per-partition vectors"):
+            nc.gpsimd.dma_start(lo_sb[:], lo.rearrange("(b p t) -> p b t", b=2, t=4))
+            nc.gpsimd.dma_start(hi_sb[:], hi.rearrange("(b p t) -> p b t", b=2, t=4))
+            nc.gpsimd.dma_start(cmin_sb[:], cmin.rearrange("(c p) -> p c", p=P))
+            nc.gpsimd.dma_start(cmax_sb[:], cmax.rearrange("(c p) -> p c", p=P))
+
+        nc.sync.dma_start(offs_sb[:], offs)
+        nc.sync.dma_start(w4_raw[:], w4_words[0].bitcast(I32))
+        load_tab(0)
+        for q in range(4):
+            nc.sync.dma_start(tab_s[32 * q + 4 : 32 * q + 12, :], tab_s32[0:2, 4 * q : 4 * q + 4, :])
+        load_w1(0, 0)
+        for r in range(4):
+            nc.sync.dma_start(tab_s[r:P:32, :], tab_s32[2, r:16:4, :])
+        load_tab(1)
+        nc.sync.dma_start(offs2_sb[:], offs2)
+        for q in range(4):
+            nc.sync.dma_start(tab2_s[32 * q + 8 : 32 * q + 16, :], tab2_s32[:, 4 * q : 4 * q + 4, :])
+        nc.sync.dma_start(tab2_w[:], tab2_words.rearrange("a p t i -> p a (t i)").bitcast(I32))
+        load_w1(1, 0)
+        load_tab(2)
+        load_w1(0, 1)
+        load_w1(1, 1)
+        nc.sync.dma_start(gain_sb[:], gain.partition_broadcast(P))
+
+        w4_w = held([P, 2 * H], U8, "w4_w")
+        w4_s = held([P, H], U8, "w4_s")
+        nc.vector.tensor_copy(
+            out=w4_w[:].bitcast(U16).rearrange("p (b t m) -> p b t m", b=2, t=4),
+            in_=w4_raw[:].bitcast(U16).rearrange("p (b m t) -> p b t m", b=2, t=4),
+        )
+        nc.vector.tensor_copy(
+            out=w4_s[:].rearrange("p (b t m) -> p b t m", b=2, t=4),
+            in_=w4s_raw[:].bitcast(U8).rearrange("p (b m t) -> p b t m", b=2, t=4),
+        )
+
+        v_w = [held([P, S], U32, "v_w%d" % a) for a in range(3)]
+        v_s = held([P, S], U8, "v_s")
+        v2_w = [held([P, S2], U32, "v2_w%d" % b) for b in range(2)]
+        v2_s = held([P, S2], U8, "v2_s")
+        w1_bf = {key: held([P, 4 * N], BF16, "w1_bf%d%d" % key) for key in w1_raw}
+        w1_w = {key: held([P, N], U32, "w1_w%d%d" % key) for key in w1_raw}
+        w1_s = {key: held([P, N], U8, "w1_s%d%d" % key) for key in w1_raw}
+
+        def cast_w1(a, b):
+            nc.scalar.copy(
+                out=w1_bf[a, b][:].rearrange("p (t m j) -> p m j t", t=4, j=4),
+                in_=w1_raw[a, b][:].rearrange("p j (m t) -> p m j t", t=4),
+            )
+
+        def quantise_w1(a, b):
+            nc.vector.quantize_mx(out=w1_w[a, b][:].bitcast(FP8X4), scales=w1_s[a, b][:], in_=w1_bf[a, b][:])
+
+        def gather_words(a, j0, j1):
+            nc.vector.tensor_copy(
+                out=v_w[a][:, j0:j1], in_=tab_w[a][:].bitcast(U32).indirect(offs_sb[:, j0 // 16 : j1 // 16])
+            )
+
+        acc = {}
+
+        def project(a, b, u):
+            cols = slice(N * u, N * (u + 1))
+            for t in range(4):
+                if a == 0:
+                    acc[b, u, t] = psum.tile([P, N], F32, name="bank")
+                if a < 2:
+                    lhs = w1_w[a, b][:, P * t : P * (t + 1)].bitcast(FP8X4)
+                    lhs_s = w1_s[a, b][:, P * t : P * (t + 1)]
+                    rhs_s = v_s[4 * a + 4 : P, cols]
+                else:
+                    c0 = N * b + P * t
+                    lhs = w4_w[:, 2 * c0 : 2 * (c0 + P)].bitcast(FP4X4)
+                    lhs_s = w4_s[:, c0 : c0 + P]
+                    rhs_s = v_s[:, cols]
+                nc.tensor.matmul_mx(
+                    out=acc[b, u, t][:], lhsT=lhs, lhsT_scale=lhs_s, rhs=v_w[a][:, cols].bitcast(FP8X4), rhs_scale=rhs_s,
+                    start=(a == 0), stop=(a == last_pass[b]),
+                )
+
+        last_pass = {0: 2, 1: 1}
+        h_rows = {(b, u): held([P, 4, N], BF16, "h_rows%d%d" % (b, u)) for b in range(2) for u in range(2)}
+        h_bf = {key: held([P, N, 4], BF16, "h_bf%d%d" % key) for key in h_rows}
+        h_w = {key: held([P, N], U32, "h_w%d%d" % key) for key in h_rows}
+        h_s = {key: held([P, N], U8, "h_s%d%d" % key) for key in h_rows}
+
+        def clip_h(b, u):
+            for t in range(4):
+                nc.vector.tensor_scalar(
+                    out=h_rows[b, u][:, t, :], in0=acc[b, u, t][:], scalar1=lo_sb[:, b, t : t + 1],
+                    scalar2=hi_sb[:, b, t : t + 1], op0=ALU.max, op1=ALU.min,
+                )
+
+        def interleave_h(b, u):
+            nc.scalar.copy(
+                out=h_bf[b, u][:].rearrange("p (c i) t -> p c t i", i=4),
+                in_=h_rows[b, u][:].rearrange("p t (c i) -> p c t i", i=4),
+            )
+
+        def quantise_h(b, u):
+            nc.vector.quantize_mx(
+                out=h_w[b, u][:].bitcast(FP8X4), scales=h_s[b, u][:], in_=h_bf[b, u][:].rearrange("p n t -> p (n t)")
+            )
+
+        def commands(u):
+            cols = slice(N * u, N * (u + 1))
+            for c in range(4):
+                y = psum.tile([P, N], F32, name="bank")
+                for b in range(2):
+                    nc.tensor.matmul_mx(
+                        out=y[:], lhsT=v2_w[b][:, P * c : P * (c + 1)].bitcast(FP8X4),
+                        lhsT_scale=v2_s[4 * b + 8 : P, P * c : P * (c + 1)],
+                        rhs=h_w[b, u][:].bitcast(FP8X4), rhs_scale=h_s[b, u][:], start=(b == 0), stop=(b == 1),
+                    )
+                scaled = held([P, N], F32, "scaled%d%d" % (u, c))
+                res = held([P, N], F32, "res%d%d" % (u, c))
+                nc.vector.tensor_tensor(out=scaled[:], in0=y[:], in1=gain_sb[:, cols], op=ALU.mult)
+                nc.vector.tensor_scalar(
+                    out=res[:], in0=scaled[:], scalar1=cmin_sb[:, c : c + 1], scalar2=cmax_sb[:, c : c + 1],
+                    op0=ALU.max, op1=ALU.min,
+                )
+                nc.sync.dma_start(out[P * c : P * (c + 1), cols], res[:])
+
+        gather_words(0, 0, S)
+        cast_w1(0, 0)
+        nc.vector.tensor_copy(out=v_s[:], in_=tab_s[:].bitcast(U8).indirect(offs_sb[:]))
+        gather_words(1, 0, S)
+        quantise_w1(0, 0)
+        project(0, 0, 0)
+        project(0, 0, 1)
+        nc.vector.tensor_copy(out=v2_s[:], in_=tab2_s[:].bitcast(U8).indirect(offs2_sb[:]))
+        for b in range(2):
+            nc.vector.tensor_copy(out=v2_w[b][:], in_=tab2_w[:, b, :].bitcast(U32).indirect(offs2_sb[:]))
+        cast_w1(1, 0)
+        gather_words(2, 0, N)
+        quantise_w1(1, 0)
+        project(1, 0, 0)
+        project(2, 0, 0)
+        gather_words(2, N, S)
+        project(1, 0, 1)
+        project(2, 0, 1)
+        cast_w1(0, 1)
+        cast_w1(1, 1)
+        clip_h(0, 0)
+        quantise_w1(0, 1)
+        interleave_h(0, 0)
+        project(0, 1, 0)
+        project(2, 1, 0)
+        clip_h(0, 1)
+        quantise_w1(1, 1)
+        interleave_h(0, 1)
+        project(1, 1, 0)
+        project(0, 1, 1)
+        project(2, 1, 1)
+        project(1, 1, 1)
+        clip_h(1, 0)
+        interleave_h(1, 0)
+        quantise_h(0, 0)
+        clip_h(1, 1)
+        interleave_h(1, 1)
+        quantise_h(0, 1)
+        quantise_h(1, 0)
+        commands(0)
+        quantise_h(1, 1)
+        commands(1)

@@ -33,7 +33,7 @@ def tile_list_clamped_actuator_commands_kernel(
         offs2_sb = keep.tile([P, S2 // 16], U16, name="offs2_sb")
         tab_w = [held([P, T], I32, "tab_w%d" % a) for a in range(3)]
         tab_s = held([P, T // 4], I32, "tab_s")
-        tab2_w = held([P, 2, T2], I32, "tab2_w")
+        tab2_w = [held([P, T2], I32, "tab2_w%d" % b) for b in range(2)]
         tab2_s = held([P, T2 // 4], I32, "tab2_s")
         w4_raw = held([P, H // 2], I32, "w4_raw")
         w4s_raw = held([P, H // 4], I32, "w4s_raw")
@@ -51,6 +51,9 @@ def tile_list_clamped_actuator_commands_kernel(
         def load_tab(a):
             nc.sync.dma_start(tab_w[a][:], tab_words[a].rearrange("p t i -> p (t i)").bitcast(I32))
 
+        def load_tab2(b):
+            nc.sync.dma_start(tab2_w[b][:], tab2_words[b].rearrange("p t i -> p (t i)").bitcast(I32))
+
         def load_w1(a, b):
             rows = w1[512 * a : 512 * (a + 1), N * b : N * (b + 1)]
             nc.sync.dma_start(w1_raw[a, b][:], rows.rearrange("(p j) c -> p j c", j=4))
@@ -59,31 +62,31 @@ def tile_list_clamped_actuator_commands_kernel(
         tab2_s32 = tab2_scales.bitcast(I32)
         w4_s32 = w4_scales.bitcast(I32)
 
-        for r in range(4):
-            nc.gpsimd.dma_start(w4s_raw[r:P:32, :], w4_s32[0, r:16:4, :])
-        with nc.allow_non_contiguous_dma(reason="short per-partition vectors"):
-            nc.gpsimd.dma_start(lo_sb[:], lo.rearrange("(b p t) -> p b t", b=2, t=4))
-            nc.gpsimd.dma_start(hi_sb[:], hi.rearrange("(b p t) -> p b t", b=2, t=4))
-            nc.gpsimd.dma_start(cmin_sb[:], cmin.rearrange("(c p) -> p c", p=P))
-            nc.gpsimd.dma_start(cmax_sb[:], cmax.rearrange("(c p) -> p c", p=P))
-
         nc.sync.dma_start(offs_sb[:], offs)
         nc.sync.dma_start(w4_raw[:], w4_words[0].bitcast(I32))
+        for r in range(4):
+            nc.sync.dma_start(w4s_raw[r:P:32, :], w4_s32[0, r:16:4, :])
         load_tab(0)
         for q in range(4):
             nc.sync.dma_start(tab_s[32 * q + 4 : 32 * q + 12, :], tab_s32[0:2, 4 * q : 4 * q + 4, :])
         load_w1(0, 0)
         for r in range(4):
             nc.sync.dma_start(tab_s[r:P:32, :], tab_s32[2, r:16:4, :])
-        load_tab(1)
+        load_tab(2)
         nc.sync.dma_start(offs2_sb[:], offs2)
+        load_tab2(0)
         for q in range(4):
             nc.sync.dma_start(tab2_s[32 * q + 8 : 32 * q + 16, :], tab2_s32[:, 4 * q : 4 * q + 4, :])
-        nc.sync.dma_start(tab2_w[:], tab2_words.rearrange("a p t i -> p a (t i)").bitcast(I32))
         load_w1(1, 0)
-        load_tab(2)
+        nc.sync.dma_start(lo_sb[:], lo.rearrange("(b p t) -> p b t", b=2, t=4))
+        nc.sync.dma_start(hi_sb[:], hi.rearrange("(b p t) -> p b t", b=2, t=4))
+        load_tab(1)
         load_w1(0, 1)
         load_w1(1, 1)
+        load_tab2(1)
+        with nc.allow_non_contiguous_dma(reason="one limit a partition"):
+            nc.sync.dma_start(cmin_sb[:], cmin.rearrange("(c p) -> p c", p=P))
+            nc.sync.dma_start(cmax_sb[:], cmax.rearrange("(c p) -> p c", p=P))
         nc.sync.dma_start(gain_sb[:], gain.partition_broadcast(P))
 
         w4_w = held([P, 2 * H], U8, "w4_w")
@@ -91,10 +94,6 @@ def tile_list_clamped_actuator_commands_kernel(
         nc.vector.tensor_copy(
             out=w4_w[:].bitcast(U16).rearrange("p (b t m) -> p b t m", b=2, t=4),
             in_=w4_raw[:].bitcast(U16).rearrange("p (b m t) -> p b t m", b=2, t=4),
-        )
-        nc.vector.tensor_copy(
-            out=w4_s[:].rearrange("p (b t m) -> p b t m", b=2, t=4),
-            in_=w4s_raw[:].bitcast(U8).rearrange("p (b m t) -> p b t m", b=2, t=4),
         )
 
         v_w = [held([P, S], U32, "v_w%d" % a) for a in range(3)]
@@ -121,10 +120,10 @@ def tile_list_clamped_actuator_commands_kernel(
 
         acc = {}
 
-        def project(a, b, u):
+        def project(passes, b, u):
             cols = slice(N * u, N * (u + 1))
-            for t in range(4):
-                if a == 0:
+            for t, a in [(t, a) for t in range(4) for a in passes]:
+                if a == first_pass[b]:
                     acc[b, u, t] = psum.tile([P, N], F32, name="bank")
                 if a < 2:
                     lhs = w1_w[a, b][:, P * t : P * (t + 1)].bitcast(FP8X4)
@@ -137,14 +136,20 @@ def tile_list_clamped_actuator_commands_kernel(
                     rhs_s = v_s[:, cols]
                 nc.tensor.matmul_mx(
                     out=acc[b, u, t][:], lhsT=lhs, lhsT_scale=lhs_s, rhs=v_w[a][:, cols].bitcast(FP8X4), rhs_scale=rhs_s,
-                    start=(a == 0), stop=(a == last_pass[b]),
+                    start=(a == first_pass[b]), stop=(a == 1),
                 )
 
-        last_pass = {0: 2, 1: 1}
+        first_pass = {0: 0, 1: 2}
         h_rows = {(b, u): held([P, 4, N], BF16, "h_rows%d%d" % (b, u)) for b in range(2) for u in range(2)}
         h_bf = {key: held([P, N, 4], BF16, "h_bf%d%d" % key) for key in h_rows}
         h_w = {key: held([P, N], U32, "h_w%d%d" % key) for key in h_rows}
         h_s = {key: held([P, N], U8, "h_s%d%d" % key) for key in h_rows}
+
+        def stage_p(b, u):
+            for t in range(4):
+                staged = held([P, N], F32, "p_sb%d%d%d" % (b, u, t))
+                nc.scalar.copy(out=staged[:], in_=acc[b, u, t][:])
+                acc[b, u, t] = staged
 
         def clip_h(b, u):
             for t in range(4):
@@ -164,64 +169,88 @@ def tile_list_clamped_actuator_commands_kernel(
                 out=h_w[b, u][:].bitcast(FP8X4), scales=h_s[b, u][:], in_=h_bf[b, u][:].rearrange("p n t -> p (n t)")
             )
 
-        def commands(u):
-            cols = slice(N * u, N * (u + 1))
+        y = {}
+        scaled = {}
+
+        def dot(u):
             for c in range(4):
-                y = psum.tile([P, N], F32, name="bank")
+                y[u, c] = psum.tile([P, N], F32, name="bank")
                 for b in range(2):
                     nc.tensor.matmul_mx(
-                        out=y[:], lhsT=v2_w[b][:, P * c : P * (c + 1)].bitcast(FP8X4),
+                        out=y[u, c][:], lhsT=v2_w[b][:, P * c : P * (c + 1)].bitcast(FP8X4),
                         lhsT_scale=v2_s[4 * b + 8 : P, P * c : P * (c + 1)],
                         rhs=h_w[b, u][:].bitcast(FP8X4), rhs_scale=h_s[b, u][:], start=(b == 0), stop=(b == 1),
                     )
-                scaled = held([P, N], F32, "scaled%d%d" % (u, c))
-                res = held([P, N], F32, "res%d%d" % (u, c))
-                nc.vector.tensor_tensor(out=scaled[:], in0=y[:], in1=gain_sb[:, cols], op=ALU.mult)
-                nc.vector.tensor_scalar(
-                    out=res[:], in0=scaled[:], scalar1=cmin_sb[:, c : c + 1], scalar2=cmax_sb[:, c : c + 1],
-                    op0=ALU.max, op1=ALU.min,
-                )
-                nc.sync.dma_start(out[P * c : P * (c + 1), cols], res[:])
 
+        def scale(u, c):
+            scaled[u, c] = held([P, N], F32, "scaled%d%d" % (u, c))
+            nc.vector.tensor_tensor(out=scaled[u, c][:], in0=y[u, c][:], in1=gain_sb[:, N * u : N * (u + 1)], op=ALU.mult)
+
+        def clamp(u, c):
+            res = held([P, N], F32, "res%d%d" % (u, c))
+            nc.vector.tensor_scalar(
+                out=res[:], in0=scaled[u, c][:], scalar1=cmin_sb[:, c : c + 1], scalar2=cmax_sb[:, c : c + 1],
+                op0=ALU.max, op1=ALU.min,
+            )
+            nc.sync.dma_start(out[P * c : P * (c + 1), N * u : N * (u + 1)], res[:])
+
+        def gather_words2(b):
+            nc.vector.tensor_copy(out=v2_w[b][:], in_=tab2_w[b][:].bitcast(U32).indirect(offs2_sb[:]))
+
+        nc.vector.tensor_copy(
+            out=w4_s[:].rearrange("p (b t m) -> p b t m", b=2, t=4),
+            in_=w4s_raw[:].bitcast(U8).rearrange("p (b m t) -> p b t m", b=2, t=4),
+        )
         gather_words(0, 0, S)
         cast_w1(0, 0)
         nc.vector.tensor_copy(out=v_s[:], in_=tab_s[:].bitcast(U8).indirect(offs_sb[:]))
-        gather_words(1, 0, S)
         quantise_w1(0, 0)
-        project(0, 0, 0)
-        project(0, 0, 1)
-        nc.vector.tensor_copy(out=v2_s[:], in_=tab2_s[:].bitcast(U8).indirect(offs2_sb[:]))
-        for b in range(2):
-            nc.vector.tensor_copy(out=v2_w[b][:], in_=tab2_w[:, b, :].bitcast(U32).indirect(offs2_sb[:]))
+        project([0], 0, 0)
+        project([0], 0, 1)
+        gather_words(2, 0, S)
+        project([2], 0, 0)
+        project([2], 0, 1)
         cast_w1(1, 0)
-        gather_words(2, 0, N)
+        gather_words2(0)
+        nc.vector.tensor_copy(out=v2_s[:], in_=tab2_s[:].bitcast(U8).indirect(offs2_sb[:]))
         quantise_w1(1, 0)
-        project(1, 0, 0)
-        project(2, 0, 0)
-        gather_words(2, N, S)
-        project(1, 0, 1)
-        project(2, 0, 1)
+        gather_words(1, 0, N)
+        project([1], 0, 0)
+        gather_words(1, N, S)
+        project([1], 0, 1)
         cast_w1(0, 1)
         cast_w1(1, 1)
         clip_h(0, 0)
+        project([2], 1, 0)
         quantise_w1(0, 1)
         interleave_h(0, 0)
-        project(0, 1, 0)
-        project(2, 1, 0)
+        project([0], 1, 0)
         clip_h(0, 1)
         quantise_w1(1, 1)
         interleave_h(0, 1)
-        project(1, 1, 0)
-        project(0, 1, 1)
-        project(2, 1, 1)
-        project(1, 1, 1)
+        project([1], 1, 0)
+        project([2, 0, 1], 1, 1)
+        quantise_h(0, 0)
         clip_h(1, 0)
         interleave_h(1, 0)
-        quantise_h(0, 0)
+        quantise_h(0, 1)
+        gather_words2(1)
+        quantise_h(1, 0)
+        dot(0)
         clip_h(1, 1)
         interleave_h(1, 1)
-        quantise_h(0, 1)
-        quantise_h(1, 0)
-        commands(0)
+        scale(0, 0)
+        scale(0, 1)
+        clamp(0, 0)
+        scale(0, 2)
+        clamp(0, 1)
         quantise_h(1, 1)
-        commands(1)
+        dot(1)
+        scale(0, 3)
+        clamp(0, 2)
+        scale(1, 0)
+        clamp(0, 3)
+        for c in range(1, 4):
+            scale(1, c)
+            clamp(1, c - 1)
+        clamp(1, 3)

@@ -62,10 +62,12 @@ def tile_list_clamped_actuator_commands_kernel(
         tab2_s32 = tab2_scales.bitcast(I32)
         w4_s32 = w4_scales.bitcast(I32)
 
-        nc.sync.dma_start(offs_sb[:], offs)
+        nc.sync.dma_start(offs2_sb[:], offs2)
+        load_tab2(0)
         nc.sync.dma_start(w4_raw[:], w4_words[0].bitcast(I32))
         for r in range(4):
             nc.sync.dma_start(w4s_raw[r:P:32, :], w4_s32[0, r:16:4, :])
+        nc.sync.dma_start(offs_sb[:], offs)
         load_tab(0)
         for q in range(4):
             nc.sync.dma_start(tab_s[32 * q + 4 : 32 * q + 12, :], tab_s32[0:2, 4 * q : 4 * q + 4, :])
@@ -73,8 +75,6 @@ def tile_list_clamped_actuator_commands_kernel(
         for r in range(4):
             nc.sync.dma_start(tab_s[r:P:32, :], tab_s32[2, r:16:4, :])
         load_tab(2)
-        nc.sync.dma_start(offs2_sb[:], offs2)
-        load_tab2(0)
         for q in range(4):
             nc.sync.dma_start(tab2_s[32 * q + 8 : 32 * q + 16, :], tab2_s32[:, 4 * q : 4 * q + 4, :])
         load_w1(1, 0)
@@ -84,17 +84,13 @@ def tile_list_clamped_actuator_commands_kernel(
         load_w1(0, 1)
         load_w1(1, 1)
         load_tab2(1)
+        nc.sync.dma_start(gain_sb[:], gain.partition_broadcast(P))
         with nc.allow_non_contiguous_dma(reason="one limit a partition"):
             nc.sync.dma_start(cmin_sb[:], cmin.rearrange("(c p) -> p c", p=P))
             nc.sync.dma_start(cmax_sb[:], cmax.rearrange("(c p) -> p c", p=P))
-        nc.sync.dma_start(gain_sb[:], gain.partition_broadcast(P))
 
         w4_w = held([P, 2 * H], U8, "w4_w")
         w4_s = held([P, H], U8, "w4_s")
-        nc.vector.tensor_copy(
-            out=w4_w[:].bitcast(U16).rearrange("p (b t m) -> p b t m", b=2, t=4),
-            in_=w4_raw[:].bitcast(U16).rearrange("p (b m t) -> p b t m", b=2, t=4),
-        )
 
         v_w = [held([P, S], U32, "v_w%d" % a) for a in range(3)]
         v_s = held([P, S], U8, "v_s")
@@ -145,8 +141,8 @@ def tile_list_clamped_actuator_commands_kernel(
         h_w = {key: held([P, N], U32, "h_w%d%d" % key) for key in h_rows}
         h_s = {key: held([P, N], U8, "h_s%d%d" % key) for key in h_rows}
 
-        def stage_p(b, u):
-            for t in range(4):
+        def stage_p(b, u, ts):
+            for t in ts:
                 staged = held([P, N], F32, "p_sb%d%d%d" % (b, u, t))
                 nc.scalar.copy(out=staged[:], in_=acc[b, u, t][:])
                 acc[b, u, t] = staged
@@ -158,10 +154,16 @@ def tile_list_clamped_actuator_commands_kernel(
                     scalar2=hi_sb[:, b, t : t + 1], op0=ALU.max, op1=ALU.min,
                 )
 
-        def interleave_h(b, u):
+        def interleave_h(b, u, n0=0):
             nc.scalar.copy(
-                out=h_bf[b, u][:].rearrange("p (c i) t -> p c t i", i=4),
-                in_=h_rows[b, u][:].rearrange("p t (c i) -> p c t i", i=4),
+                out=h_bf[b, u][:, n0:N, :].rearrange("p (c i) t -> p c t i", i=4),
+                in_=h_rows[b, u][:, :, n0:N].rearrange("p t (c i) -> p c t i", i=4),
+            )
+
+        def interleave_h_gpsimd(b, u, n1):
+            nc.gpsimd.tensor_scalar(
+                out=h_bf[b, u][:, 0:n1, :], in0=h_rows[b, u][:, :, 0:n1].rearrange("p t n -> p n t"), scalar1=1.0, scalar2=0.0,
+                op0=ALU.mult, op1=ALU.add,
             )
 
         def quantise_h(b, u):
@@ -172,15 +174,15 @@ def tile_list_clamped_actuator_commands_kernel(
         y = {}
         scaled = {}
 
-        def dot(u):
+        def dot(b, u):
             for c in range(4):
-                y[u, c] = psum.tile([P, N], F32, name="bank")
-                for b in range(2):
-                    nc.tensor.matmul_mx(
-                        out=y[u, c][:], lhsT=v2_w[b][:, P * c : P * (c + 1)].bitcast(FP8X4),
-                        lhsT_scale=v2_s[4 * b + 8 : P, P * c : P * (c + 1)],
-                        rhs=h_w[b, u][:].bitcast(FP8X4), rhs_scale=h_s[b, u][:], start=(b == 0), stop=(b == 1),
-                    )
+                if b == 0:
+                    y[u, c] = psum.tile([P, N], F32, name="bank")
+                nc.tensor.matmul_mx(
+                    out=y[u, c][:], lhsT=v2_w[b][:, P * c : P * (c + 1)].bitcast(FP8X4),
+                    lhsT_scale=v2_s[4 * b + 8 : P, P * c : P * (c + 1)],
+                    rhs=h_w[b, u][:].bitcast(FP8X4), rhs_scale=h_s[b, u][:], start=(b == 0), stop=(b == 1),
+                )
 
         def scale(u, c):
             scaled[u, c] = held([P, N], F32, "scaled%d%d" % (u, c))
@@ -197,6 +199,11 @@ def tile_list_clamped_actuator_commands_kernel(
         def gather_words2(b):
             nc.vector.tensor_copy(out=v2_w[b][:], in_=tab2_w[b][:].bitcast(U32).indirect(offs2_sb[:]))
 
+        gather_words2(0)
+        nc.vector.tensor_copy(
+            out=w4_w[:].bitcast(U16).rearrange("p (b t m) -> p b t m", b=2, t=4),
+            in_=w4_raw[:].bitcast(U16).rearrange("p (b m t) -> p b t m", b=2, t=4),
+        )
         nc.vector.tensor_copy(
             out=w4_s[:].rearrange("p (b t m) -> p b t m", b=2, t=4),
             in_=w4s_raw[:].bitcast(U8).rearrange("p (b m t) -> p b t m", b=2, t=4),
@@ -211,7 +218,6 @@ def tile_list_clamped_actuator_commands_kernel(
         project([2], 0, 0)
         project([2], 0, 1)
         cast_w1(1, 0)
-        gather_words2(0)
         nc.vector.tensor_copy(out=v2_s[:], in_=tab2_s[:].bitcast(U8).indirect(offs2_sb[:]))
         quantise_w1(1, 0)
         gather_words(1, 0, N)
@@ -221,31 +227,36 @@ def tile_list_clamped_actuator_commands_kernel(
         cast_w1(0, 1)
         cast_w1(1, 1)
         clip_h(0, 0)
+        interleave_h_gpsimd(0, 0, 384)
+        interleave_h(0, 0, 384)
         project([2], 1, 0)
-        quantise_w1(0, 1)
-        interleave_h(0, 0)
-        project([0], 1, 0)
         clip_h(0, 1)
-        quantise_w1(1, 1)
         interleave_h(0, 1)
+        project([2], 1, 1)
+        quantise_w1(0, 1)
+        project([0], 1, 0)
+        quantise_w1(1, 1)
         project([1], 1, 0)
-        project([2, 0, 1], 1, 1)
+        project([0, 1], 1, 1)
         quantise_h(0, 0)
+        stage_p(1, 1, [0, 1])
         clip_h(1, 0)
         interleave_h(1, 0)
+        dot(0, 0)
         quantise_h(0, 1)
         gather_words2(1)
-        quantise_h(1, 0)
-        dot(0)
         clip_h(1, 1)
         interleave_h(1, 1)
+        quantise_h(1, 0)
+        dot(1, 0)
+        dot(0, 1)
         scale(0, 0)
         scale(0, 1)
         clamp(0, 0)
+        quantise_h(1, 1)
+        dot(1, 1)
         scale(0, 2)
         clamp(0, 1)
-        quantise_h(1, 1)
-        dot(1)
         scale(0, 3)
         clamp(0, 2)
         scale(1, 0)

@@ -33,65 +33,64 @@ def tile_list_clamped_actuator_commands_kernel(
         offs2_sb = keep.tile([P, S2 // 16], U16, name="offs2_sb")
         tab_w = [held([P, T], I32, "tab_w%d" % a) for a in range(3)]
         tab_s = held([P, T // 4], I32, "tab_s")
-        tab2_w = [held([P, T2], I32, "tab2_w%d" % b) for b in range(2)]
+        tab2_w = {}
         tab2_s = held([P, T2 // 4], I32, "tab2_s")
         w4_raw = held([P, H // 2], I32, "w4_raw")
         w4s_raw = held([P, H // 4], I32, "w4s_raw")
         w1_raw = {(a, b): held([P, 4, N], F32, "w1_raw%d%d" % (a, b)) for a in range(2) for b in range(2)}
-        lo_sb = held([P, 2, 4], F32, "lo_sb")
-        hi_sb = held([P, 2, 4], F32, "hi_sb")
+        lo_sb = held([P, 2, 8], F32, "lo_sb")
+        hi_sb = held([P, 2, 8], F32, "hi_sb")
         cmin_sb = held([P, 4], F32, "cmin_sb")
         cmax_sb = held([P, 4], F32, "cmax_sb")
+        floor_sb = held([P, 4], F32, "floor_sb")
         gain_sb = held([P, S], F32, "gain_sb")
 
-        nc.vector.memset(w4s_raw[:], 0)
-        nc.vector.memset(tab_s[:], 0)
-        nc.vector.memset(tab2_s[:], 0)
+        tab_s32 = tab_scales.bitcast(I32)
+        tab2_s32 = tab2_scales.bitcast(I32)
+        w4_s32 = w4_scales.bitcast(I32)
 
-        def load_tab(a):
-            nc.sync.dma_start(tab_w[a][:], tab_words[a].rearrange("p t i -> p (t i)").bitcast(I32))
+        def load_tab(a, t0=0, t1=T):
+            nc.sync.dma_start(tab_w[a][:, t0:t1], tab_words[a].rearrange("p t i -> p (t i)").bitcast(I32)[:, t0:t1])
 
         def load_tab2(b):
+            tab2_w[b] = keep.tile([P, T2], I32, name="tab2_w%d" % b, tag="w1_raw%d1" % b, align_bytes=64)
             nc.sync.dma_start(tab2_w[b][:], tab2_words[b].rearrange("p t i -> p (t i)").bitcast(I32))
 
         def load_w1(a, b):
             rows = w1[512 * a : 512 * (a + 1), N * b : N * (b + 1)]
             nc.sync.dma_start(w1_raw[a, b][:], rows.rearrange("(p j) c -> p j c", j=4))
 
-        tab_s32 = tab_scales.bitcast(I32)
-        tab2_s32 = tab2_scales.bitcast(I32)
-        w4_s32 = w4_scales.bitcast(I32)
+        def load_w4(c0=0, c1=H // 2):
+            nc.sync.dma_start(w4_raw[:, c0:c1], w4_words[0].bitcast(I32)[:, c0:c1])
 
-        nc.sync.dma_start(offs2_sb[:], offs2)
-        load_tab2(0)
-        nc.sync.dma_start(w4_raw[:], w4_words[0].bitcast(I32))
-        for r in range(4):
-            nc.sync.dma_start(w4s_raw[r:P:32, :], w4_s32[0, r:16:4, :])
-        nc.sync.dma_start(offs_sb[:], offs)
-        load_tab(0)
-        for q in range(4):
-            nc.sync.dma_start(tab_s[32 * q + 4 : 32 * q + 12, :], tab_s32[0:2, 4 * q : 4 * q + 4, :])
-        load_w1(0, 0)
-        for r in range(4):
-            nc.sync.dma_start(tab_s[r:P:32, :], tab_s32[2, r:16:4, :])
-        load_tab(2)
-        for q in range(4):
-            nc.sync.dma_start(tab2_s[32 * q + 8 : 32 * q + 16, :], tab2_s32[:, 4 * q : 4 * q + 4, :])
-        load_w1(1, 0)
-        nc.sync.dma_start(lo_sb[:], lo.rearrange("(b p t) -> p b t", b=2, t=4))
-        nc.sync.dma_start(hi_sb[:], hi.rearrange("(b p t) -> p b t", b=2, t=4))
-        load_tab(1)
-        load_w1(0, 1)
-        load_w1(1, 1)
-        load_tab2(1)
-        nc.sync.dma_start(gain_sb[:], gain.partition_broadcast(P))
-        with nc.allow_non_contiguous_dma(reason="one limit a partition"):
-            nc.sync.dma_start(cmin_sb[:], cmin.rearrange("(c p) -> p c", p=P))
-            nc.sync.dma_start(cmax_sb[:], cmax.rearrange("(c p) -> p c", p=P))
+        def load_w4_scales(rs):
+            for r in rs:
+                nc.sync.dma_start(w4s_raw[r:P:32, :], w4_s32[0, r:16:4, :])
+
+        def load_tab_scales_w1(qs):
+            for q in qs:
+                nc.sync.dma_start(tab_s[32 * q + 4 : 32 * q + 12, :], tab_s32[0:2, 4 * q : 4 * q + 4, :])
+
+        def load_tab_scales_w4(rs):
+            for r in rs:
+                nc.sync.dma_start(tab_s[r:P:32, :], tab_s32[2, r:16:4, :])
+
+        def load_tab2_scales(qs):
+            for q in qs:
+                nc.sync.dma_start(tab2_s[32 * q + 8 : 32 * q + 16, :], tab2_s32[:, 4 * q : 4 * q + 4, :])
+
+        def load_limits():
+            nc.sync.dma_start(lo_sb[:, :, 0:4], lo.rearrange("(b p t) -> p b t", b=2, t=4))
+            nc.sync.dma_start(hi_sb[:, :, 0:4], hi.rearrange("(b p t) -> p b t", b=2, t=4))
+
+        def load_finish():
+            nc.sync.dma_start(gain_sb[:], gain.partition_broadcast(P))
+            with nc.allow_non_contiguous_dma(reason="one limit a partition"):
+                nc.sync.dma_start(cmin_sb[:], cmin.rearrange("(c p) -> p c", p=P))
+                nc.sync.dma_start(cmax_sb[:], cmax.rearrange("(c p) -> p c", p=P))
 
         w4_w = held([P, 2 * H], U8, "w4_w")
         w4_s = held([P, H], U8, "w4_s")
-
         v_w = [held([P, S], U32, "v_w%d" % a) for a in range(3)]
         v_s = held([P, S], U8, "v_s")
         v2_w = [held([P, S2], U32, "v2_w%d" % b) for b in range(2)]
@@ -100,11 +99,31 @@ def tile_list_clamped_actuator_commands_kernel(
         w1_w = {key: held([P, N], U32, "w1_w%d%d" % key) for key in w1_raw}
         w1_s = {key: held([P, N], U8, "w1_s%d%d" % key) for key in w1_raw}
 
-        def cast_w1(a, b):
-            nc.scalar.copy(
-                out=w1_bf[a, b][:].rearrange("p (t m j) -> p m j t", t=4, j=4),
-                in_=w1_raw[a, b][:].rearrange("p j (m t) -> p m j t", t=4),
+        def deal_w4_words():
+            nc.vector.tensor_copy(
+                out=w4_w[:].bitcast(U16).rearrange("p (b t m) -> p b t m", b=2, t=4),
+                in_=w4_raw[:].bitcast(U16).rearrange("p (b m t) -> p b t m", b=2, t=4),
             )
+
+        def deal_w4_scales():
+            nc.vector.tensor_copy(
+                out=w4_s[:].rearrange("p (b t m) -> p b t m", b=2, t=4),
+                in_=w4s_raw[:].bitcast(U8).rearrange("p (b m t) -> p b t m", b=2, t=4),
+            )
+
+        def cast_views(a, b):
+            return (
+                w1_bf[a, b][:].rearrange("p (t m j) -> p m j t", t=4, j=4),
+                w1_raw[a, b][:].rearrange("p j (m t) -> p m j t", t=4),
+            )
+
+        def cast_w1(a, b, m0=0, m1=P):
+            dst, raw = cast_views(a, b)
+            nc.scalar.copy(out=dst[:, m0:m1], in_=raw[:, m0:m1])
+
+        def cast_w1_vector(a, b, m0=0, m1=P):
+            dst, raw = cast_views(a, b)
+            nc.vector.tensor_copy(out=dst[:, m0:m1], in_=raw[:, m0:m1])
 
         def quantise_w1(a, b):
             nc.vector.quantize_mx(out=w1_w[a, b][:].bitcast(FP8X4), scales=w1_s[a, b][:], in_=w1_bf[a, b][:])
@@ -114,11 +133,21 @@ def tile_list_clamped_actuator_commands_kernel(
                 out=v_w[a][:, j0:j1], in_=tab_w[a][:].bitcast(U32).indirect(offs_sb[:, j0 // 16 : j1 // 16])
             )
 
-        acc = {}
+        def gather_scales():
+            nc.vector.tensor_copy(out=v_s[:], in_=tab_s[:].bitcast(U8).indirect(offs_sb[:]))
 
-        def project(passes, b, u):
+        def gather_words2(b):
+            nc.vector.tensor_copy(out=v2_w[b][:], in_=tab2_w[b][:].bitcast(U32).indirect(offs2_sb[:]))
+
+        def gather_scales2():
+            nc.vector.tensor_copy(out=v2_s[:], in_=tab2_s[:].bitcast(U8).indirect(offs2_sb[:]))
+
+        acc = {}
+        first_pass = {0: 0, 1: 2}
+
+        def project(order, b, u):
             cols = slice(N * u, N * (u + 1))
-            for t, a in [(t, a) for t in range(4) for a in passes]:
+            for t, a in order:
                 if a == first_pass[b]:
                     acc[b, u, t] = psum.tile([P, N], F32, name="bank")
                 if a < 2:
@@ -135,36 +164,50 @@ def tile_list_clamped_actuator_commands_kernel(
                     start=(a == first_pass[b]), stop=(a == 1),
                 )
 
-        first_pass = {0: 0, 1: 2}
-        h_rows = {(b, u): held([P, 4, N], BF16, "h_rows%d%d" % (b, u)) for b in range(2) for u in range(2)}
-        h_bf = {key: held([P, N, 4], BF16, "h_bf%d%d" % key) for key in h_rows}
-        h_w = {key: held([P, N], U32, "h_w%d%d" % key) for key in h_rows}
-        h_s = {key: held([P, N], U8, "h_s%d%d" % key) for key in h_rows}
+        def by_pass(passes):
+            return [(t, a) for a in passes for t in range(4)]
 
-        def stage_p(b, u, ts):
+        def by_bank(passes):
+            return [(t, a) for t in range(4) for a in passes]
+
+        keys = [(b, u) for b in range(2) for u in range(2)]
+        p_rows = {key: [held([P, N], BF16, "p_rows%d%d%d" % (key + (t,))) for t in range(4)] for key in keys}
+        h_rows = {key: held([P, 4, N], BF16, "h_rows%d%d" % key) for key in keys}
+        h_bf = {key: held([P, N, 4], BF16, "h_bf%d%d" % key) for key in keys}
+        h_w = {key: held([P, N], U32, "h_w%d%d" % key) for key in keys}
+        h_s = {key: held([P, N], U8, "h_s%d%d" % key) for key in keys}
+
+        def round_p(b, u, ts=range(4)):
             for t in ts:
-                staged = held([P, N], F32, "p_sb%d%d%d" % (b, u, t))
-                nc.scalar.copy(out=staged[:], in_=acc[b, u, t][:])
-                acc[b, u, t] = staged
+                nc.scalar.copy(out=p_rows[b, u][t][:], in_=acc[b, u, t][:])
 
-        def clip_h(b, u):
-            for t in range(4):
-                nc.vector.tensor_scalar(
-                    out=h_rows[b, u][:, t, :], in0=acc[b, u, t][:], scalar1=lo_sb[:, b, t : t + 1],
-                    scalar2=hi_sb[:, b, t : t + 1], op0=ALU.max, op1=ALU.min,
-                )
-
-        def interleave_h(b, u, n0=0):
-            nc.scalar.copy(
-                out=h_bf[b, u][:, n0:N, :].rearrange("p (c i) t -> p c t i", i=4),
-                in_=h_rows[b, u][:, :, n0:N].rearrange("p t (c i) -> p c t i", i=4),
+        def clip(b, u, t, source):
+            nc.vector.tensor_scalar(
+                out=h_rows[b, u][:, t, :], in0=source, scalar1=lo_sb[:, b, t : t + 1],
+                scalar2=hi_sb[:, b, t : t + 1], op0=ALU.max, op1=ALU.min,
             )
 
-        def interleave_h_gpsimd(b, u, n1):
-            nc.gpsimd.tensor_scalar(
-                out=h_bf[b, u][:, 0:n1, :], in0=h_rows[b, u][:, :, 0:n1].rearrange("p t n -> p n t"), scalar1=1.0, scalar2=0.0,
-                op0=ALU.mult, op1=ALU.add,
+        def clip_h(b, u, ts=range(4)):
+            for t in ts:
+                clip(b, u, t, p_rows[b, u][t][:])
+
+        def clip_bank(b, u, ts):
+            for t in ts:
+                clip(b, u, t, acc[b, u, t][:])
+
+        def weave_views(b, u, n0, n1):
+            return (
+                h_bf[b, u][:, n0:n1, :].rearrange("p (c i) t -> p c t i", i=4),
+                h_rows[b, u][:, :, n0:n1].rearrange("p t (c i) -> p c t i", i=4),
             )
+
+        def weave(b, u, n0=0, n1=N):
+            dst, rows = weave_views(b, u, n0, n1)
+            nc.vector.tensor_copy(out=dst, in_=rows)
+
+        def weave_scalar(b, u, n0=0, n1=N):
+            dst, rows = weave_views(b, u, n0, n1)
+            nc.scalar.copy(out=dst, in_=rows)
 
         def quantise_h(b, u):
             nc.vector.quantize_mx(
@@ -174,8 +217,8 @@ def tile_list_clamped_actuator_commands_kernel(
         y = {}
         scaled = {}
 
-        def dot(b, u):
-            for c in range(4):
+        def dot(u, order):
+            for c, b in order:
                 if b == 0:
                     y[u, c] = psum.tile([P, N], F32, name="bank")
                 nc.tensor.matmul_mx(
@@ -188,80 +231,100 @@ def tile_list_clamped_actuator_commands_kernel(
             scaled[u, c] = held([P, N], F32, "scaled%d%d" % (u, c))
             nc.vector.tensor_tensor(out=scaled[u, c][:], in0=y[u, c][:], in1=gain_sb[:, N * u : N * (u + 1)], op=ALU.mult)
 
-        def clamp(u, c):
+        def order_limits():
+            nc.vector.tensor_tensor(out=floor_sb[:], in0=cmin_sb[:], in1=cmax_sb[:], op=ALU.min)
+
+        def clamp(u, c, engine):
             res = held([P, N], F32, "res%d%d" % (u, c))
-            nc.vector.tensor_scalar(
-                out=res[:], in0=scaled[u, c][:], scalar1=cmin_sb[:, c : c + 1], scalar2=cmax_sb[:, c : c + 1],
-                op0=ALU.max, op1=ALU.min,
+            engine.tensor_scalar(
+                out=res[:], in0=scaled[u, c][:], scalar1=cmax_sb[:, c : c + 1], scalar2=floor_sb[:, c : c + 1],
+                op0=ALU.min, op1=ALU.max,
             )
             nc.sync.dma_start(out[P * c : P * (c + 1), N * u : N * (u + 1)], res[:])
 
-        def gather_words2(b):
-            nc.vector.tensor_copy(out=v2_w[b][:], in_=tab2_w[b][:].bitcast(U32).indirect(offs2_sb[:]))
+        nc.vector.memset(tab_s[:], 0)
+        nc.vector.memset(w4s_raw[:], 0)
+        nc.gpsimd.memset(tab2_s[:], 0)
 
-        gather_words2(0)
-        nc.vector.tensor_copy(
-            out=w4_w[:].bitcast(U16).rearrange("p (b t m) -> p b t m", b=2, t=4),
-            in_=w4_raw[:].bitcast(U16).rearrange("p (b m t) -> p b t m", b=2, t=4),
-        )
-        nc.vector.tensor_copy(
-            out=w4_s[:].rearrange("p (b t m) -> p b t m", b=2, t=4),
-            in_=w4s_raw[:].bitcast(U8).rearrange("p (b m t) -> p b t m", b=2, t=4),
-        )
+        load_w4(0, H // 4)
+        load_w4(H // 4, H // 2)
+        nc.sync.dma_start(offs_sb[:], offs)
+        load_limits()
+        nc.sync.dma_start(offs2_sb[:], offs2)
+        load_tab(0, 0, T // 2)
+        load_tab(0, T // 2, T)
+        load_tab_scales_w1(range(4))
+        load_tab_scales_w4(range(1))
+        load_w1(0, 0)
+        load_tab_scales_w4(range(1, 4))
+        load_tab(2)
+        load_w4_scales(range(4))
+        load_w1(1, 0)
+        load_tab2_scales(range(4))
+        load_tab(1)
+        load_w1(0, 1)
+        load_w1(1, 1)
+        load_finish()
+
+        deal_w4_words()
         gather_words(0, 0, S)
-        cast_w1(0, 0)
-        nc.vector.tensor_copy(out=v_s[:], in_=tab_s[:].bitcast(U8).indirect(offs_sb[:]))
+        cast_w1(0, 0, 0, 96)
+        cast_w1_vector(0, 0, 96, P)
+        gather_scales()
         quantise_w1(0, 0)
-        project([0], 0, 0)
-        project([0], 0, 1)
+        project(by_pass([0]), 0, 0)
+        project(by_pass([0]), 0, 1)
         gather_words(2, 0, S)
-        project([2], 0, 0)
-        project([2], 0, 1)
+        deal_w4_scales()
+        project(by_pass([2]), 0, 0)
+        project(by_pass([2]), 0, 1)
         cast_w1(1, 0)
-        nc.vector.tensor_copy(out=v2_s[:], in_=tab2_s[:].bitcast(U8).indirect(offs2_sb[:]))
-        quantise_w1(1, 0)
+        gather_scales2()
         gather_words(1, 0, N)
-        project([1], 0, 0)
+        quantise_w1(1, 0)
+        project(by_pass([1]), 0, 0)
         gather_words(1, N, S)
-        project([1], 0, 1)
-        cast_w1(0, 1)
-        cast_w1(1, 1)
-        clip_h(0, 0)
-        interleave_h_gpsimd(0, 0, 384)
-        interleave_h(0, 0, 384)
-        project([2], 1, 0)
-        clip_h(0, 1)
-        interleave_h(0, 1)
-        project([2], 1, 1)
+        project(by_pass([1]), 0, 1)
+        round_p(0, 0)
+        cast_w1_vector(0, 1)
+        load_tab2(0)
+        project(by_pass([2]), 1, 0)
+        clip_h(0, 0, range(2))
         quantise_w1(0, 1)
-        project([0], 1, 0)
+        project(by_pass([0]), 1, 0)
+        cast_w1_vector(1, 1)
+        load_tab2(1)
+        clip_h(0, 0, range(2, 4))
         quantise_w1(1, 1)
-        project([1], 1, 0)
-        project([0, 1], 1, 1)
+        project(by_pass([1]), 1, 0)
+        round_p(0, 1)
+        weave_scalar(0, 0, 0, N // 2)
+        round_p(1, 0)
+        project(by_bank([2, 0, 1]), 1, 1)
+        round_p(1, 1)
+        clip_h(0, 1)
+        weave(0, 0, N // 2, N)
+        weave_scalar(0, 1)
+        gather_words2(0)
         quantise_h(0, 0)
-        stage_p(1, 1, [0, 1])
         clip_h(1, 0)
-        interleave_h(1, 0)
-        dot(0, 0)
-        quantise_h(0, 1)
         gather_words2(1)
+        weave(1, 0)
         clip_h(1, 1)
-        interleave_h(1, 1)
         quantise_h(1, 0)
-        dot(1, 0)
-        dot(0, 1)
-        scale(0, 0)
-        scale(0, 1)
-        clamp(0, 0)
-        quantise_h(1, 1)
-        dot(1, 1)
-        scale(0, 2)
-        clamp(0, 1)
-        scale(0, 3)
-        clamp(0, 2)
+        dot(0, by_pass([0, 1]))
+        weave_scalar(1, 1, 0, N // 2)
+        weave(1, 1, N // 2, N)
+        order_limits()
+        for c in range(4):
+            scale(0, c)
+            clamp(0, c, nc.gpsimd)
+            if c < 2:
+                quantise_h(c, 1)
+            if c == 1:
+                dot(1, by_pass([0, 1]))
         scale(1, 0)
-        clamp(0, 3)
         for c in range(1, 4):
             scale(1, c)
-            clamp(1, c - 1)
-        clamp(1, 3)
+            clamp(1, c - 1, nc.vector)
+        clamp(1, 3, nc.vector)

@@ -69,7 +69,7 @@ def tile_list_clamped_actuator_commands_kernel(
 
         def load_tab_scales_w1(qs):
             for q in qs:
-                nc.sync.dma_start(tab_s[32 * q + 4 : 32 * q + 12, :], tab_s32[0:2, 4 * q : 4 * q + 4, :])
+                nc.gpsimd.dma_start(tab_s[32 * q + 4 : 32 * q + 12, :], tab_s32[0:2, 4 * q : 4 * q + 4, :])
 
         def load_tab_scales_w4(rs):
             for r in rs:
@@ -227,36 +227,37 @@ def tile_list_clamped_actuator_commands_kernel(
                     rhs=h_w[b, u][:].bitcast(FP8X4), rhs_scale=h_s[b, u][:], start=(b == 0), stop=(b == 1),
                 )
 
-        def scale(u, c):
-            scaled[u, c] = held([P, N], F32, "scaled%d%d" % (u, c))
-            nc.vector.tensor_tensor(out=scaled[u, c][:], in0=y[u, c][:], in1=gain_sb[:, N * u : N * (u + 1)], op=ALU.mult)
+        def scale(u, c, n0=0, n1=N):
+            scaled[u, c, n0] = held([P, n1 - n0], F32, "scaled%d%d_%d" % (u, c, n0))
+            nc.vector.tensor_tensor(
+                out=scaled[u, c, n0][:], in0=y[u, c][:, n0:n1], in1=gain_sb[:, N * u + n0 : N * u + n1], op=ALU.mult
+            )
 
         def order_limits():
             nc.vector.tensor_tensor(out=floor_sb[:], in0=cmin_sb[:], in1=cmax_sb[:], op=ALU.min)
 
-        def clamp(u, c, engine):
-            res = held([P, N], F32, "res%d%d" % (u, c))
+        def clamp(u, c, engine, n0=0, n1=N):
+            res = held([P, n1 - n0], F32, "res%d%d_%d" % (u, c, n0))
             engine.tensor_scalar(
-                out=res[:], in0=scaled[u, c][:], scalar1=cmax_sb[:, c : c + 1], scalar2=floor_sb[:, c : c + 1],
+                out=res[:], in0=scaled[u, c, n0][:], scalar1=cmax_sb[:, c : c + 1], scalar2=floor_sb[:, c : c + 1],
                 op0=ALU.min, op1=ALU.max,
             )
-            nc.sync.dma_start(out[P * c : P * (c + 1), N * u : N * (u + 1)], res[:])
+            nc.sync.dma_start(out[P * c : P * (c + 1), N * u + n0 : N * u + n1], res[:])
 
         nc.vector.memset(tab_s[:], 0)
         nc.vector.memset(w4s_raw[:], 0)
-        nc.gpsimd.memset(tab2_s[:], 0)
+        nc.vector.memset(tab2_s[:], 0)
+        load_tab_scales_w1(range(4))
 
-        load_w4(0, H // 4)
-        load_w4(H // 4, H // 2)
         nc.sync.dma_start(offs_sb[:], offs)
-        load_limits()
-        nc.sync.dma_start(offs2_sb[:], offs2)
         load_tab(0, 0, T // 2)
         load_tab(0, T // 2, T)
-        load_tab_scales_w1(range(4))
-        load_tab_scales_w4(range(1))
+        load_w4(0, H // 4)
+        load_w4(H // 4, H // 2)
+        load_limits()
+        nc.sync.dma_start(offs2_sb[:], offs2)
         load_w1(0, 0)
-        load_tab_scales_w4(range(1, 4))
+        load_tab_scales_w4(range(4))
         load_tab(2)
         load_w4_scales(range(4))
         load_w1(1, 0)
@@ -266,8 +267,8 @@ def tile_list_clamped_actuator_commands_kernel(
         load_w1(1, 1)
         load_finish()
 
-        deal_w4_words()
         gather_words(0, 0, S)
+        deal_w4_words()
         cast_w1(0, 0, 0, 96)
         cast_w1_vector(0, 0, 96, P)
         gather_scales()

@@ -173,7 +173,7 @@ def tile_list_clamped_actuator_commands_kernel(
         keys = [(b, u) for b in range(2) for u in range(2)]
         p_rows = {key: [held([P, N], BF16, "p_rows%d%d%d" % (key + (t,))) for t in range(4)] for key in keys}
         h_rows = {key: held([P, 4, N], BF16, "h_rows%d%d" % key) for key in keys}
-        h_bf = {key: held([P, N, 4], BF16, "h_bf%d%d" % key) for key in keys}
+        h_bf = {key: held([P, N, 4], BF16, "h_bf%d%d" % key) for key in keys if key != (0, 1)}
         h_w = {key: held([P, N], U32, "h_w%d%d" % key) for key in keys}
         h_s = {key: held([P, N], U8, "h_s%d%d" % key) for key in keys}
 
@@ -208,6 +208,12 @@ def tile_list_clamped_actuator_commands_kernel(
         def weave_scalar(b, u, n0=0, n1=N):
             dst, rows = weave_views(b, u, n0, n1)
             nc.scalar.copy(out=dst, in_=rows)
+
+        def weave_gpsimd(b, u, n0=0, n1=N):
+            nc.gpsimd.tensor_scalar(
+                out=h_bf[b, u][:, n0:n1, :], in0=h_rows[b, u][:, :, n0:n1].rearrange("p t n -> p n t"),
+                scalar1=1.0, scalar2=0.0, op0=ALU.mult, op1=ALU.add,
+            )
 
         def quantise_h(b, u):
             nc.vector.quantize_mx(
@@ -249,29 +255,31 @@ def tile_list_clamped_actuator_commands_kernel(
         nc.vector.memset(tab2_s[:], 0)
         load_tab_scales_w1(range(4))
 
-        nc.sync.dma_start(offs_sb[:], offs)
-        load_tab(0, 0, T // 2)
-        load_tab(0, T // 2, T)
         load_w4(0, H // 4)
         load_w4(H // 4, H // 2)
+        nc.sync.dma_start(offs_sb[:], offs)
         load_limits()
         nc.sync.dma_start(offs2_sb[:], offs2)
-        load_w1(0, 0)
+        load_tab(0, 0, T // 2)
+        load_tab(0, T // 2, T)
         load_tab_scales_w4(range(4))
+        load_w1(0, 0)
+        load_w4_scales(range(2))
         load_tab(2)
-        load_w4_scales(range(4))
+        load_w4_scales(range(2, 4))
+        load_tab2_scales(range(2))
         load_w1(1, 0)
-        load_tab2_scales(range(4))
+        load_tab2_scales(range(2, 4))
         load_tab(1)
         load_w1(0, 1)
         load_w1(1, 1)
         load_finish()
 
-        gather_words(0, 0, S)
         deal_w4_words()
+        gather_words(0, 0, S)
         cast_w1(0, 0, 0, 96)
-        cast_w1_vector(0, 0, 96, P)
         gather_scales()
+        cast_w1_vector(0, 0, 96, P)
         quantise_w1(0, 0)
         project(by_pass([0]), 0, 0)
         project(by_pass([0]), 0, 1)
@@ -305,10 +313,11 @@ def tile_list_clamped_actuator_commands_kernel(
         round_p(1, 1)
         clip_h(0, 1)
         weave(0, 0, N // 2, N)
-        weave_scalar(0, 1)
         gather_words2(0)
         quantise_h(0, 0)
         clip_h(1, 0)
+        h_bf[0, 1] = keep.tile([P, N, 4], BF16, name="h_bf01", tag="p_rows103", align_bytes=64)
+        weave_scalar(0, 1)
         gather_words2(1)
         weave(1, 0)
         clip_h(1, 1)

@@ -24,6 +24,7 @@ def tile_list_clamped_actuator_commands_kernel(
     nc = tc.nc
     with ExitStack() as ctx:
         keep = ctx.enter_context(tc.tile_pool(name="keep", bufs=1))
+        shared = ctx.enter_context(tc.tile_pool(name="shared", bufs=1))
         psum = ctx.enter_context(tc.psum_pool(name="psum", bufs=8))
 
         def held(shape, dtype, name):
@@ -33,7 +34,7 @@ def tile_list_clamped_actuator_commands_kernel(
         offs2_sb = keep.tile([P, S2 // 16], U16, name="offs2_sb")
         tab_w = [held([P, T], I32, "tab_w%d" % a) for a in range(3)]
         tab_s = held([P, T // 4], I32, "tab_s")
-        tab2_w = {}
+        tab2_w = [held([P, T2], I32, "tab2_w%d" % b) for b in range(2)]
         tab2_s = held([P, T2 // 4], I32, "tab2_s")
         w4_raw = held([P, H // 2], I32, "w4_raw")
         w4s_raw = held([P, H // 4], I32, "w4s_raw")
@@ -42,7 +43,7 @@ def tile_list_clamped_actuator_commands_kernel(
         hi_sb = held([P, 2, 8], F32, "hi_sb")
         cmin_sb = held([P, 4], F32, "cmin_sb")
         cmax_sb = held([P, 4], F32, "cmax_sb")
-        floor_sb = held([P, 4], F32, "floor_sb")
+        late = {}
         gain_sb = held([P, S], F32, "gain_sb")
 
         tab_s32 = tab_scales.bitcast(I32)
@@ -53,7 +54,6 @@ def tile_list_clamped_actuator_commands_kernel(
             nc.sync.dma_start(tab_w[a][:, t0:t1], tab_words[a].rearrange("p t i -> p (t i)").bitcast(I32)[:, t0:t1])
 
         def load_tab2(b):
-            tab2_w[b] = keep.tile([P, T2], I32, name="tab2_w%d" % b, tag="w1_raw%d1" % b, align_bytes=64)
             nc.sync.dma_start(tab2_w[b][:], tab2_words[b].rearrange("p t i -> p (t i)").bitcast(I32))
 
         def load_w1(a, b):
@@ -84,18 +84,19 @@ def tile_list_clamped_actuator_commands_kernel(
             nc.sync.dma_start(hi_sb[:, :, 0:4], hi.rearrange("(b p t) -> p b t", b=2, t=4))
 
         def load_finish():
-            nc.sync.dma_start(gain_sb[:], gain.partition_broadcast(P))
             with nc.allow_non_contiguous_dma(reason="one limit a partition"):
                 nc.sync.dma_start(cmin_sb[:], cmin.rearrange("(c p) -> p c", p=P))
                 nc.sync.dma_start(cmax_sb[:], cmax.rearrange("(c p) -> p c", p=P))
+            nc.sync.dma_start(gain_sb[:], gain.partition_broadcast(P))
 
         w4_w = held([P, 2 * H], U8, "w4_w")
         w4_s = held([P, H], U8, "w4_s")
         v_w = [held([P, S], U32, "v_w%d" % a) for a in range(3)]
         v_s = held([P, S], U8, "v_s")
-        v2_w = [held([P, S2], U32, "v2_w%d" % b) for b in range(2)]
+        v2_w = {1: held([P, S2], U32, "v2_w1")}
         v2_s = held([P, S2], U8, "v2_s")
-        w1_bf = {key: held([P, 4 * N], BF16, "w1_bf%d%d" % key) for key in w1_raw}
+        w1_bf = {key: held([P, 4 * N], BF16, "w1_bf%d%d" % key) for key in w1_raw if key != (1, 1)}
+        w1_bf[1, 1] = shared.tile([P, 4 * N], BF16, name="w1_bf11", align_bytes=64, offset=0)
         w1_w = {key: held([P, N], U32, "w1_w%d%d" % key) for key in w1_raw}
         w1_s = {key: held([P, N], U8, "w1_s%d%d" % key) for key in w1_raw}
 
@@ -172,8 +173,8 @@ def tile_list_clamped_actuator_commands_kernel(
 
         keys = [(b, u) for b in range(2) for u in range(2)]
         p_rows = {key: [held([P, N], BF16, "p_rows%d%d%d" % (key + (t,))) for t in range(4)] for key in keys}
-        h_rows = {key: held([P, 4, N], BF16, "h_rows%d%d" % key) for key in keys}
-        h_bf = {key: held([P, N, 4], BF16, "h_bf%d%d" % key) for key in keys if key != (0, 1)}
+        h_rows = {key: held([P, 4, N], BF16, "h_rows%d%d" % key) for key in keys if key != (0, 1)}
+        h_bf = {(1, u): held([P, N, 4], BF16, "h_bf1%d" % u) for u in range(2)}
         h_w = {key: held([P, N], U32, "h_w%d%d" % key) for key in keys}
         h_s = {key: held([P, N], U8, "h_s%d%d" % key) for key in keys}
 
@@ -240,12 +241,13 @@ def tile_list_clamped_actuator_commands_kernel(
             )
 
         def order_limits():
-            nc.vector.tensor_tensor(out=floor_sb[:], in0=cmin_sb[:], in1=cmax_sb[:], op=ALU.min)
+            late["floor"] = keep.tile([P, 4], F32, name="floor", tag="p_rows110", align_bytes=64)
+            nc.vector.tensor_tensor(out=late["floor"][:], in0=cmin_sb[:], in1=cmax_sb[:], op=ALU.min)
 
         def clamp(u, c, engine, n0=0, n1=N):
             res = held([P, n1 - n0], F32, "res%d%d_%d" % (u, c, n0))
             engine.tensor_scalar(
-                out=res[:], in0=scaled[u, c, n0][:], scalar1=cmax_sb[:, c : c + 1], scalar2=floor_sb[:, c : c + 1],
+                out=res[:], in0=scaled[u, c, n0][:], scalar1=cmax_sb[:, c : c + 1], scalar2=late["floor"][:, c : c + 1],
                 op0=ALU.min, op1=ALU.max,
             )
             nc.sync.dma_start(out[P * c : P * (c + 1), N * u + n0 : N * u + n1], res[:])
@@ -273,6 +275,8 @@ def tile_list_clamped_actuator_commands_kernel(
         load_tab(1)
         load_w1(0, 1)
         load_w1(1, 1)
+        load_tab2(0)
+        load_tab2(1)
         load_finish()
 
         deal_w4_words()
@@ -296,29 +300,30 @@ def tile_list_clamped_actuator_commands_kernel(
         project(by_pass([1]), 0, 1)
         round_p(0, 0)
         cast_w1_vector(0, 1)
-        load_tab2(0)
         project(by_pass([2]), 1, 0)
         clip_h(0, 0, range(2))
         quantise_w1(0, 1)
         project(by_pass([0]), 1, 0)
         cast_w1_vector(1, 1)
-        load_tab2(1)
         clip_h(0, 0, range(2, 4))
         quantise_w1(1, 1)
         project(by_pass([1]), 1, 0)
         round_p(0, 1)
-        weave_scalar(0, 0, 0, N // 2)
+        v2_w[0] = shared.tile([P, S2], U32, name="v2_w0", align_bytes=64, offset=0)
+        h_bf[0, 0] = shared.tile([P, N, 4], BF16, name="h_bf00", align_bytes=64, offset=4 * S2)
+        weave_scalar(0, 0, 0, P)
+        weave_gpsimd(0, 0, P, N)
         round_p(1, 0)
         project(by_bank([2, 0, 1]), 1, 1)
         round_p(1, 1)
-        clip_h(0, 1)
-        weave(0, 0, N // 2, N)
         gather_words2(0)
-        quantise_h(0, 0)
+        gather_words2(1)
         clip_h(1, 0)
+        h_rows[0, 1] = keep.tile([P, 4, N], BF16, name="h_rows01", tag="tab2_w0", align_bytes=64)
+        clip_h(0, 1)
         h_bf[0, 1] = keep.tile([P, N, 4], BF16, name="h_bf01", tag="p_rows103", align_bytes=64)
         weave_scalar(0, 1)
-        gather_words2(1)
+        quantise_h(0, 0)
         weave(1, 0)
         clip_h(1, 1)
         quantise_h(1, 0)

@@ -13,9 +13,14 @@ FP4X4 = mybir.dt.float4_e2m1fn_x4
 ALU = mybir.AluOpType
 
 P = 128
-K, KX, KE, H, T, S, T2, S2 = 1536, 1024, 512, 1024, 2048, 1024, 1024, 512
+K, H, T, S, T2, S2 = 1536, 1024, 2048, 1024, 1024, 512
 N = 512
+W4_PASS = 2
 FLOPS = 2 * K * H * S + 2 * H * S2 * S
+
+SCALAR_QUADS = (96, 80)
+SCALAR_STATES_FIRST = 128
+SCALAR_STATES_LAST = 256
 
 
 def tile_list_clamped_actuator_commands_kernel(
@@ -30,6 +35,9 @@ def tile_list_clamped_actuator_commands_kernel(
         def held(shape, dtype, name):
             return keep.tile(shape, dtype, name=name, align_bytes=64)
 
+        def reused(shape, dtype, name, after):
+            return keep.tile(shape, dtype, name=name, tag=after, align_bytes=64)
+
         offs_sb = keep.tile([P, S // 16], U16, name="offs_sb")
         offs2_sb = keep.tile([P, S2 // 16], U16, name="offs2_sb")
         tab_w = [held([P, T], I32, "tab_w%d" % a) for a in range(3)]
@@ -43,7 +51,6 @@ def tile_list_clamped_actuator_commands_kernel(
         hi_sb = held([P, 2, 8], F32, "hi_sb")
         cmin_sb = held([P, 4], F32, "cmin_sb")
         cmax_sb = held([P, 4], F32, "cmax_sb")
-        late = {}
         gain_sb = held([P, S], F32, "gain_sb")
 
         tab_s32 = tab_scales.bitcast(I32)
@@ -57,37 +64,12 @@ def tile_list_clamped_actuator_commands_kernel(
             nc.sync.dma_start(tab2_w[b][:], tab2_words[b].rearrange("p t i -> p (t i)").bitcast(I32))
 
         def load_w1(a, b):
-            rows = w1[512 * a : 512 * (a + 1), N * b : N * (b + 1)]
+            rows = w1[N * a : N * (a + 1), N * b : N * (b + 1)]
             nc.sync.dma_start(w1_raw[a, b][:], rows.rearrange("(p j) c -> p j c", j=4))
 
-        def load_w4(c0=0, c1=H // 2):
-            nc.sync.dma_start(w4_raw[:, c0:c1], w4_words[0].bitcast(I32)[:, c0:c1])
-
-        def load_w4_scales(rs):
-            for r in rs:
-                nc.sync.dma_start(w4s_raw[r:P:32, :], w4_s32[0, r:16:4, :])
-
-        def load_tab_scales_w1(qs):
-            for q in qs:
-                nc.gpsimd.dma_start(tab_s[32 * q + 4 : 32 * q + 12, :], tab_s32[0:2, 4 * q : 4 * q + 4, :])
-
-        def load_tab_scales_w4(rs):
-            for r in rs:
-                nc.sync.dma_start(tab_s[r:P:32, :], tab_s32[2, r:16:4, :])
-
-        def load_tab2_scales(qs):
-            for q in qs:
+        def load_tab2_scales(quadrants):
+            for q in quadrants:
                 nc.sync.dma_start(tab2_s[32 * q + 8 : 32 * q + 16, :], tab2_s32[:, 4 * q : 4 * q + 4, :])
-
-        def load_limits():
-            nc.sync.dma_start(lo_sb[:, :, 0:4], lo.rearrange("(b p t) -> p b t", b=2, t=4))
-            nc.sync.dma_start(hi_sb[:, :, 0:4], hi.rearrange("(b p t) -> p b t", b=2, t=4))
-
-        def load_finish():
-            with nc.allow_non_contiguous_dma(reason="one limit a partition"):
-                nc.sync.dma_start(cmin_sb[:], cmin.rearrange("(c p) -> p c", p=P))
-                nc.sync.dma_start(cmax_sb[:], cmax.rearrange("(c p) -> p c", p=P))
-            nc.sync.dma_start(gain_sb[:], gain.partition_broadcast(P))
 
         w4_w = held([P, 2 * H], U8, "w4_w")
         w4_s = held([P, H], U8, "w4_s")
@@ -100,120 +82,88 @@ def tile_list_clamped_actuator_commands_kernel(
         w1_w = {key: held([P, N], U32, "w1_w%d%d" % key) for key in w1_raw}
         w1_s = {key: held([P, N], U8, "w1_s%d%d" % key) for key in w1_raw}
 
-        def deal_w4_words():
+        def deal(dst, src):
             nc.vector.tensor_copy(
-                out=w4_w[:].bitcast(U16).rearrange("p (b t m) -> p b t m", b=2, t=4),
-                in_=w4_raw[:].bitcast(U16).rearrange("p (b m t) -> p b t m", b=2, t=4),
+                out=dst.rearrange("p (b t m) -> p b t m", b=2, t=4), in_=src.rearrange("p (b m t) -> p b t m", b=2, t=4)
             )
 
-        def deal_w4_scales():
-            nc.vector.tensor_copy(
-                out=w4_s[:].rearrange("p (b t m) -> p b t m", b=2, t=4),
-                in_=w4s_raw[:].bitcast(U8).rearrange("p (b m t) -> p b t m", b=2, t=4),
-            )
-
-        def cast_views(a, b):
+        def cast_views(a, b, order):
             return (
-                w1_bf[a, b][:].rearrange("p (t m j) -> p m j t", t=4, j=4),
-                w1_raw[a, b][:].rearrange("p j (m t) -> p m j t", t=4),
+                w1_bf[a, b][:].rearrange("p (t m j) -> p " + order, t=4, j=4),
+                w1_raw[a, b][:].rearrange("p j (m t) -> p " + order, t=4),
             )
 
-        def cast_w1(a, b, m0=0, m1=P):
-            dst, raw = cast_views(a, b)
-            nc.scalar.copy(out=dst[:, m0:m1], in_=raw[:, m0:m1])
+        def cast_shared(a):
+            split = SCALAR_QUADS[a]
+            dst, raw = cast_views(a, 0, "m j t")
+            nc.scalar.copy(out=dst[:, 0:split], in_=raw[:, 0:split])
+            dst, raw = cast_views(a, 0, "t m j")
+            gpsimd_copy(dst[:, :, split:P], raw[:, :, split:P])
 
-        def cast_w1_vector(a, b, m0=0, m1=P):
-            dst, raw = cast_views(a, b)
-            nc.vector.tensor_copy(out=dst[:, m0:m1], in_=raw[:, m0:m1])
+        def cast_vector(a):
+            dst, raw = cast_views(a, 1, "m j t")
+            nc.vector.tensor_copy(out=dst, in_=raw)
+
+        def gpsimd_copy(dst, src):
+            nc.gpsimd.tensor_scalar(out=dst, in0=src, scalar1=1.0, scalar2=0.0, op0=ALU.mult, op1=ALU.add)
 
         def quantise_w1(a, b):
             nc.vector.quantize_mx(out=w1_w[a, b][:].bitcast(FP8X4), scales=w1_s[a, b][:], in_=w1_bf[a, b][:])
 
+        def gather(dst, window, offsets):
+            nc.vector.tensor_copy(out=dst, in_=window.indirect(offsets))
+
         def gather_words(a, j0, j1):
-            nc.vector.tensor_copy(
-                out=v_w[a][:, j0:j1], in_=tab_w[a][:].bitcast(U32).indirect(offs_sb[:, j0 // 16 : j1 // 16])
-            )
-
-        def gather_scales():
-            nc.vector.tensor_copy(out=v_s[:], in_=tab_s[:].bitcast(U8).indirect(offs_sb[:]))
-
-        def gather_words2(b):
-            nc.vector.tensor_copy(out=v2_w[b][:], in_=tab2_w[b][:].bitcast(U32).indirect(offs2_sb[:]))
-
-        def gather_scales2():
-            nc.vector.tensor_copy(out=v2_s[:], in_=tab2_s[:].bitcast(U8).indirect(offs2_sb[:]))
+            gather(v_w[a][:, j0:j1], tab_w[a][:].bitcast(U32), offs_sb[:, j0 // 16 : j1 // 16])
 
         acc = {}
-        first_pass = {0: 0, 1: 2}
+        passes_done = {}
 
-        def project(order, b, u):
+        def project(b, u, steps):
             cols = slice(N * u, N * (u + 1))
-            for t, a in order:
-                if a == first_pass[b]:
+            for t, a in steps:
+                passes_done[b, u, t] = passes_done.get((b, u, t), 0) + 1
+                if passes_done[b, u, t] == 1:
                     acc[b, u, t] = psum.tile([P, N], F32, name="bank")
-                if a < 2:
-                    lhs = w1_w[a, b][:, P * t : P * (t + 1)].bitcast(FP8X4)
-                    lhs_s = w1_s[a, b][:, P * t : P * (t + 1)]
-                    rhs_s = v_s[4 * a + 4 : P, cols]
-                else:
+                if a == W4_PASS:
                     c0 = N * b + P * t
                     lhs = w4_w[:, 2 * c0 : 2 * (c0 + P)].bitcast(FP4X4)
                     lhs_s = w4_s[:, c0 : c0 + P]
                     rhs_s = v_s[:, cols]
+                else:
+                    lhs = w1_w[a, b][:, P * t : P * (t + 1)].bitcast(FP8X4)
+                    lhs_s = w1_s[a, b][:, P * t : P * (t + 1)]
+                    rhs_s = v_s[4 * a + 4 : P, cols]
                 nc.tensor.matmul_mx(
                     out=acc[b, u, t][:], lhsT=lhs, lhsT_scale=lhs_s, rhs=v_w[a][:, cols].bitcast(FP8X4), rhs_scale=rhs_s,
-                    start=(a == first_pass[b]), stop=(a == 1),
+                    start=(passes_done[b, u, t] == 1), stop=(passes_done[b, u, t] == 3),
                 )
 
-        def by_pass(passes):
-            return [(t, a) for a in passes for t in range(4)]
+        def one_pass(a):
+            return [(t, a) for t in range(4)]
 
-        def by_bank(passes):
-            return [(t, a) for t in range(4) for a in passes]
-
-        keys = [(b, u) for b in range(2) for u in range(2)]
-        p_rows = {key: [held([P, N], BF16, "p_rows%d%d%d" % (key + (t,))) for t in range(4)] for key in keys}
-        h_rows = {key: held([P, 4, N], BF16, "h_rows%d%d" % key) for key in keys if key != (0, 1)}
+        groups = [(b, u) for b in range(2) for u in range(2)]
+        p_rows = {g: [held([P, N], BF16, "p_rows%d%d%d" % (g + (t,))) for t in range(4)] for g in groups}
+        h_rows = {(1, u): held([P, 4, N], BF16, "h_rows1%d" % u) for u in range(2)}
         h_bf = {(1, u): held([P, N, 4], BF16, "h_bf1%d" % u) for u in range(2)}
-        h_w = {key: held([P, N], U32, "h_w%d%d" % key) for key in keys}
-        h_s = {key: held([P, N], U8, "h_s%d%d" % key) for key in keys}
+        h_w = {g: held([P, N], U32, "h_w%d%d" % g) for g in groups}
+        h_s = {g: held([P, N], U8, "h_s%d%d" % g) for g in groups}
 
-        def round_p(b, u, ts=range(4)):
-            for t in ts:
+        def round_p(b, u):
+            for t in range(4):
                 nc.scalar.copy(out=p_rows[b, u][t][:], in_=acc[b, u, t][:])
 
-        def clip(b, u, t, source):
-            nc.vector.tensor_scalar(
-                out=h_rows[b, u][:, t, :], in0=source, scalar1=lo_sb[:, b, t : t + 1],
-                scalar2=hi_sb[:, b, t : t + 1], op0=ALU.max, op1=ALU.min,
-            )
+        def clip(b, u, banks=range(4)):
+            for t in banks:
+                nc.vector.tensor_scalar(
+                    out=h_rows[b, u][:, t, :], in0=p_rows[b, u][t][:], scalar1=lo_sb[:, b, t : t + 1],
+                    scalar2=hi_sb[:, b, t : t + 1], op0=ALU.max, op1=ALU.min,
+                )
 
-        def clip_h(b, u, ts=range(4)):
-            for t in ts:
-                clip(b, u, t, p_rows[b, u][t][:])
-
-        def clip_bank(b, u, ts):
-            for t in ts:
-                clip(b, u, t, acc[b, u, t][:])
-
-        def weave_views(b, u, n0, n1):
-            return (
-                h_bf[b, u][:, n0:n1, :].rearrange("p (c i) t -> p c t i", i=4),
-                h_rows[b, u][:, :, n0:n1].rearrange("p t (c i) -> p c t i", i=4),
-            )
-
-        def weave(b, u, n0=0, n1=N):
-            dst, rows = weave_views(b, u, n0, n1)
-            nc.vector.tensor_copy(out=dst, in_=rows)
-
-        def weave_scalar(b, u, n0=0, n1=N):
-            dst, rows = weave_views(b, u, n0, n1)
-            nc.scalar.copy(out=dst, in_=rows)
-
-        def weave_gpsimd(b, u, n0=0, n1=N):
-            nc.gpsimd.tensor_scalar(
-                out=h_bf[b, u][:, n0:n1, :], in0=h_rows[b, u][:, :, n0:n1].rearrange("p t n -> p n t"),
-                scalar1=1.0, scalar2=0.0, op0=ALU.mult, op1=ALU.add,
+        def weave(copy, b, u, n0=0, n1=N):
+            copy(
+                out=h_bf[b, u][:, n0:n1, :].rearrange("p (c i) t -> p c t i", i=4),
+                in_=h_rows[b, u][:, :, n0:n1].rearrange("p t (c i) -> p c t i", i=4),
             )
 
         def quantise_h(b, u):
@@ -224,51 +174,49 @@ def tile_list_clamped_actuator_commands_kernel(
         y = {}
         scaled = {}
 
-        def dot(u, order):
-            for c, b in order:
-                if b == 0:
-                    y[u, c] = psum.tile([P, N], F32, name="bank")
-                nc.tensor.matmul_mx(
-                    out=y[u, c][:], lhsT=v2_w[b][:, P * c : P * (c + 1)].bitcast(FP8X4),
-                    lhsT_scale=v2_s[4 * b + 8 : P, P * c : P * (c + 1)],
-                    rhs=h_w[b, u][:].bitcast(FP8X4), rhs_scale=h_s[b, u][:], start=(b == 0), stop=(b == 1),
-                )
+        def dot(u):
+            for b in range(2):
+                for c in range(4):
+                    if b == 0:
+                        y[u, c] = psum.tile([P, N], F32, name="bank")
+                    nc.tensor.matmul_mx(
+                        out=y[u, c][:], lhsT=v2_w[b][:, P * c : P * (c + 1)].bitcast(FP8X4),
+                        lhsT_scale=v2_s[4 * b + 8 : P, P * c : P * (c + 1)],
+                        rhs=h_w[b, u][:].bitcast(FP8X4), rhs_scale=h_s[b, u][:], start=(b == 0), stop=(b == 1),
+                    )
 
-        def scale(u, c, n0=0, n1=N):
-            scaled[u, c, n0] = held([P, n1 - n0], F32, "scaled%d%d_%d" % (u, c, n0))
-            nc.vector.tensor_tensor(
-                out=scaled[u, c, n0][:], in0=y[u, c][:, n0:n1], in1=gain_sb[:, N * u + n0 : N * u + n1], op=ALU.mult
-            )
+        def scale(u, c):
+            scaled[u, c] = held([P, N], F32, "scaled%d%d" % (u, c))
+            nc.vector.tensor_tensor(out=scaled[u, c][:], in0=y[u, c][:], in1=gain_sb[:, N * u : N * (u + 1)], op=ALU.mult)
 
-        def order_limits():
-            late["floor"] = keep.tile([P, 4], F32, name="floor", tag="p_rows110", align_bytes=64)
-            nc.vector.tensor_tensor(out=late["floor"][:], in0=cmin_sb[:], in1=cmax_sb[:], op=ALU.min)
-
-        def clamp(u, c, engine, n0=0, n1=N):
-            res = held([P, n1 - n0], F32, "res%d%d_%d" % (u, c, n0))
+        def clamp_and_store(engine, floor, u, c):
+            res = held([P, N], F32, "res%d%d" % (u, c))
             engine.tensor_scalar(
-                out=res[:], in0=scaled[u, c, n0][:], scalar1=cmax_sb[:, c : c + 1], scalar2=late["floor"][:, c : c + 1],
+                out=res[:], in0=scaled[u, c][:], scalar1=cmax_sb[:, c : c + 1], scalar2=floor[:, c : c + 1],
                 op0=ALU.min, op1=ALU.max,
             )
-            nc.sync.dma_start(out[P * c : P * (c + 1), N * u + n0 : N * u + n1], res[:])
+            nc.sync.dma_start(out[P * c : P * (c + 1), N * u : N * (u + 1)], res[:])
 
         nc.vector.memset(tab_s[:], 0)
         nc.vector.memset(w4s_raw[:], 0)
         nc.vector.memset(tab2_s[:], 0)
-        load_tab_scales_w1(range(4))
-
-        load_w4(0, H // 4)
-        load_w4(H // 4, H // 2)
+        for q in range(4):
+            nc.gpsimd.dma_start(tab_s[32 * q + 4 : 32 * q + 12, :], tab_s32[0:2, 4 * q : 4 * q + 4, :])
+        for half in range(2):
+            words = slice(half * H // 4, (half + 1) * H // 4)
+            nc.sync.dma_start(w4_raw[:, words], w4_words[0].bitcast(I32)[:, words])
         nc.sync.dma_start(offs_sb[:], offs)
-        load_limits()
+        nc.sync.dma_start(lo_sb[:, :, 0:4], lo.rearrange("(b p t) -> p b t", b=2, t=4))
+        nc.sync.dma_start(hi_sb[:, :, 0:4], hi.rearrange("(b p t) -> p b t", b=2, t=4))
         nc.sync.dma_start(offs2_sb[:], offs2)
         load_tab(0, 0, T // 2)
         load_tab(0, T // 2, T)
-        load_tab_scales_w4(range(4))
+        for r in range(4):
+            nc.sync.dma_start(tab_s[r:P:32, :], tab_s32[W4_PASS, r:16:4, :])
         load_w1(0, 0)
-        load_w4_scales(range(2))
-        load_tab(2)
-        load_w4_scales(range(2, 4))
+        for r in range(4):
+            nc.sync.dma_start(w4s_raw[r:P:32, :], w4_s32[0, r:16:4, :])
+        load_tab(W4_PASS)
         load_tab2_scales(range(2))
         load_w1(1, 0)
         load_tab2_scales(range(2, 4))
@@ -277,69 +225,79 @@ def tile_list_clamped_actuator_commands_kernel(
         load_w1(1, 1)
         load_tab2(0)
         load_tab2(1)
-        load_finish()
+        with nc.allow_non_contiguous_dma(reason="one limit a partition"):
+            nc.sync.dma_start(cmin_sb[:], cmin.rearrange("(c p) -> p c", p=P))
+            nc.sync.dma_start(cmax_sb[:], cmax.rearrange("(c p) -> p c", p=P))
+        nc.sync.dma_start(gain_sb[:], gain.partition_broadcast(P))
 
-        deal_w4_words()
+        deal(w4_w[:].bitcast(U16), w4_raw[:].bitcast(U16))
         gather_words(0, 0, S)
-        cast_w1(0, 0, 0, 96)
-        gather_scales()
-        cast_w1_vector(0, 0, 96, P)
+        cast_shared(0)
+        gather(v_s[:], tab_s[:].bitcast(U8), offs_sb[:])
+        deal(w4_s[:], w4s_raw[:].bitcast(U8))
         quantise_w1(0, 0)
-        project(by_pass([0]), 0, 0)
-        project(by_pass([0]), 0, 1)
-        gather_words(2, 0, S)
-        deal_w4_scales()
-        project(by_pass([2]), 0, 0)
-        project(by_pass([2]), 0, 1)
-        cast_w1(1, 0)
-        gather_scales2()
-        gather_words(1, 0, N)
+        for u in range(2):
+            project(0, u, one_pass(0))
+        gather_words(W4_PASS, 0, S)
+        for u in range(2):
+            project(0, u, one_pass(W4_PASS))
+        cast_shared(1)
+        gather(v2_s[:], tab2_s[:].bitcast(U8), offs2_sb[:])
         quantise_w1(1, 0)
-        project(by_pass([1]), 0, 0)
-        gather_words(1, N, S)
-        project(by_pass([1]), 0, 1)
+        for u in range(2):
+            gather_words(1, N * u, N * (u + 1))
+            project(0, u, one_pass(1))
+
         round_p(0, 0)
-        cast_w1_vector(0, 1)
-        project(by_pass([2]), 1, 0)
-        clip_h(0, 0, range(2))
+        cast_vector(0)
+        project(1, 0, one_pass(W4_PASS))
         quantise_w1(0, 1)
-        project(by_pass([0]), 1, 0)
-        cast_w1_vector(1, 1)
-        clip_h(0, 0, range(2, 4))
+        h_rows[0, 0] = reused([P, 4, N], BF16, "h_rows00", "w1_raw01")
+        clip(0, 0, range(2))
+        project(1, 0, one_pass(0))
+        cast_vector(1)
+        clip(0, 0, range(2, 4))
         quantise_w1(1, 1)
-        project(by_pass([1]), 1, 0)
+        project(1, 0, one_pass(1))
         round_p(0, 1)
+
         v2_w[0] = shared.tile([P, S2], U32, name="v2_w0", align_bytes=64, offset=0)
         h_bf[0, 0] = shared.tile([P, N, 4], BF16, name="h_bf00", align_bytes=64, offset=4 * S2)
-        weave_scalar(0, 0, 0, P)
-        weave_gpsimd(0, 0, P, N)
+        weave(nc.scalar.copy, 0, 0, 0, SCALAR_STATES_FIRST)
+        gpsimd_copy(
+            h_bf[0, 0][:, SCALAR_STATES_FIRST:N, :],
+            h_rows[0, 0][:, :, SCALAR_STATES_FIRST:N].rearrange("p t n -> p n t"),
+        )
         round_p(1, 0)
-        project(by_bank([2, 0, 1]), 1, 1)
+        early, late = (W4_PASS, 0, 1), (1, W4_PASS, 0)
+        project(1, 1, [(t, a) for t in range(4) for a in (early if t < 2 else late)])
         round_p(1, 1)
-        gather_words2(0)
-        gather_words2(1)
-        clip_h(1, 0)
-        h_rows[0, 1] = keep.tile([P, 4, N], BF16, name="h_rows01", tag="tab2_w0", align_bytes=64)
-        clip_h(0, 1)
-        h_bf[0, 1] = keep.tile([P, N, 4], BF16, name="h_bf01", tag="p_rows103", align_bytes=64)
-        weave_scalar(0, 1)
+        for b in range(2):
+            gather(v2_w[b][:], tab2_w[b][:].bitcast(U32), offs2_sb[:])
+        clip(1, 0)
+        h_rows[0, 1] = reused([P, 4, N], BF16, "h_rows01", "tab2_w0")
+        clip(0, 1)
+        h_bf[0, 1] = reused([P, N, 4], BF16, "h_bf01", "p_rows103")
+        weave(nc.scalar.copy, 0, 1)
         quantise_h(0, 0)
-        weave(1, 0)
-        clip_h(1, 1)
+        weave(nc.vector.tensor_copy, 1, 0)
+        clip(1, 1)
         quantise_h(1, 0)
-        dot(0, by_pass([0, 1]))
-        weave_scalar(1, 1, 0, N // 2)
-        weave(1, 1, N // 2, N)
-        order_limits()
+        dot(0)
+        weave(nc.scalar.copy, 1, 1, 0, SCALAR_STATES_LAST)
+        weave(nc.vector.tensor_copy, 1, 1, SCALAR_STATES_LAST, N)
+
+        floor = reused([P, 4], F32, "floor", "p_rows110")
+        nc.vector.tensor_tensor(out=floor[:], in0=cmin_sb[:], in1=cmax_sb[:], op=ALU.min)
         for c in range(4):
             scale(0, c)
-            clamp(0, c, nc.gpsimd)
+            clamp_and_store(nc.gpsimd, floor, 0, c)
             if c < 2:
                 quantise_h(c, 1)
             if c == 1:
-                dot(1, by_pass([0, 1]))
+                dot(1)
         scale(1, 0)
         for c in range(1, 4):
             scale(1, c)
-            clamp(1, c - 1, nc.vector)
-        clamp(1, 3, nc.vector)
+            clamp_and_store(nc.vector, floor, 1, c - 1)
+        clamp_and_store(nc.vector, floor, 1, 3)

@@ -19,8 +19,7 @@ W4_PASS = 2
 FLOPS = 2 * K * H * S + 2 * H * S2 * S
 
 SCALAR_QUADS = (96, 80)
-SCALAR_STATES_FIRST = 128
-SCALAR_STATES_LAST = 256
+SCALAR_STATES_SECOND = 384
 
 
 def tile_list_clamped_actuator_commands_kernel(
@@ -46,7 +45,9 @@ def tile_list_clamped_actuator_commands_kernel(
         tab2_s = held([P, T2 // 4], I32, "tab2_s")
         w4_raw = held([P, H // 2], I32, "w4_raw")
         w4s_raw = held([P, H // 4], I32, "w4s_raw")
-        w1_raw = {(a, b): held([P, 4, N], F32, "w1_raw%d%d" % (a, b)) for a in range(2) for b in range(2)}
+        blocks = [(a, b) for a in range(2) for b in range(2)]
+        w1_raw = {key: held([P, 4, N], F32, "w1_raw%d%d" % key) for key in blocks[1:]}
+        first_raw = [held([P, 4, N // 2], F32, "first_raw%d" % half) for half in range(2)]
         lo_sb = held([P, 2, 8], F32, "lo_sb")
         hi_sb = held([P, 2, 8], F32, "hi_sb")
         cmin_sb = held([P, 4], F32, "cmin_sb")
@@ -72,15 +73,14 @@ def tile_list_clamped_actuator_commands_kernel(
                 nc.sync.dma_start(tab2_s[32 * q + 8 : 32 * q + 16, :], tab2_s32[:, 4 * q : 4 * q + 4, :])
 
         w4_w = held([P, 2 * H], U8, "w4_w")
-        w4_s = held([P, H], U8, "w4_s")
         v_w = [held([P, S], U32, "v_w%d" % a) for a in range(3)]
         v_s = held([P, S], U8, "v_s")
-        v2_w = {1: held([P, S2], U32, "v2_w1")}
+        v2_w = {}
         v2_s = held([P, S2], U8, "v2_s")
-        w1_bf = {key: held([P, 4 * N], BF16, "w1_bf%d%d" % key) for key in w1_raw if key != (1, 1)}
+        w1_bf = {key: held([P, 4 * N], BF16, "w1_bf%d%d" % key) for key in blocks[:3]}
         w1_bf[1, 1] = shared.tile([P, 4 * N], BF16, name="w1_bf11", align_bytes=64, offset=0)
-        w1_w = {key: held([P, N], U32, "w1_w%d%d" % key) for key in w1_raw}
-        w1_s = {key: held([P, N], U8, "w1_s%d%d" % key) for key in w1_raw}
+        w1_w = {key: held([P, N], U32, "w1_w%d%d" % key) for key in blocks}
+        w1_s = {key: held([P, N], U8, "w1_s%d%d" % key) for key in blocks}
 
         def deal(dst, src):
             nc.vector.tensor_copy(
@@ -99,6 +99,16 @@ def tile_list_clamped_actuator_commands_kernel(
             nc.scalar.copy(out=dst[:, 0:split], in_=raw[:, 0:split])
             dst, raw = cast_views(a, 0, "t m j")
             gpsimd_copy(dst[:, :, split:P], raw[:, :, split:P])
+
+        def cast_first():
+            split = SCALAR_QUADS[0]
+            dst = w1_bf[0, 0][:].rearrange("p (t m j) -> p m j t", t=4, j=4)
+            raw = [tile[:].rearrange("p j (m t) -> p m j t", t=4) for tile in first_raw]
+            nc.scalar.copy(out=dst[:, 0 : P // 2], in_=raw[0])
+            nc.scalar.copy(out=dst[:, P // 2 : split], in_=raw[1][:, 0 : split - P // 2])
+            dst = w1_bf[0, 0][:].rearrange("p (t m j) -> p t m j", t=4, j=4)
+            raw = first_raw[1][:].rearrange("p j (m t) -> p t m j", t=4)
+            gpsimd_copy(dst[:, :, split:P], raw[:, :, split - P // 2 : P // 2])
 
         def cast_vector(a):
             dst, raw = cast_views(a, 1, "m j t")
@@ -145,8 +155,8 @@ def tile_list_clamped_actuator_commands_kernel(
         groups = [(b, u) for b in range(2) for u in range(2)]
         p_rows = {g: [held([P, N], BF16, "p_rows%d%d%d" % (g + (t,))) for t in range(4)] for g in groups}
         h_rows = {(1, u): held([P, 4, N], BF16, "h_rows1%d" % u) for u in range(2)}
-        h_bf = {(1, u): held([P, N, 4], BF16, "h_bf1%d" % u) for u in range(2)}
-        h_w = {g: held([P, N], U32, "h_w%d%d" % g) for g in groups}
+        h_bf = {g: held([P, N, 4], BF16, "h_bf%d%d" % g) for g in groups[1:]}
+        h_w = {g: held([P, N], U32, "h_w%d%d" % g) for g in groups[1:]}
         h_s = {g: held([P, N], U8, "h_s%d%d" % g) for g in groups}
 
         def round_p(b, u):
@@ -160,10 +170,16 @@ def tile_list_clamped_actuator_commands_kernel(
                     scalar2=hi_sb[:, b, t : t + 1], op0=ALU.max, op1=ALU.min,
                 )
 
+        def weave_into(copy, dst, rows):
+            copy(out=dst.rearrange("p (c i) t -> p c t i", i=4), in_=rows.rearrange("p t (c i) -> p c t i", i=4))
+
         def weave(copy, b, u, n0=0, n1=N):
-            copy(
-                out=h_bf[b, u][:, n0:n1, :].rearrange("p (c i) t -> p c t i", i=4),
-                in_=h_rows[b, u][:, :, n0:n1].rearrange("p t (c i) -> p c t i", i=4),
+            weave_into(copy, h_bf[b, u][:, n0:n1, :], h_rows[b, u][:, :, n0:n1])
+
+        def quantise_first(woven, n0):
+            cols = slice(n0, n0 + N // 2)
+            nc.vector.quantize_mx(
+                out=h_w[0, 0][:, cols].bitcast(FP8X4), scales=h_s[0, 0][:, cols], in_=woven[:].rearrange("p n t -> p (n t)")
             )
 
         def quantise_h(b, u):
@@ -200,7 +216,7 @@ def tile_list_clamped_actuator_commands_kernel(
         nc.vector.memset(tab_s[:], 0)
         nc.vector.memset(w4s_raw[:], 0)
         nc.vector.memset(tab2_s[:], 0)
-        for q in range(4):
+        for q in range(2, 4):
             nc.gpsimd.dma_start(tab_s[32 * q + 4 : 32 * q + 12, :], tab_s32[0:2, 4 * q : 4 * q + 4, :])
         for half in range(2):
             words = slice(half * H // 4, (half + 1) * H // 4)
@@ -213,7 +229,11 @@ def tile_list_clamped_actuator_commands_kernel(
         load_tab(0, T // 2, T)
         for r in range(4):
             nc.sync.dma_start(tab_s[r:P:32, :], tab_s32[W4_PASS, r:16:4, :])
-        load_w1(0, 0)
+        for q in range(2):
+            nc.sync.dma_start(tab_s[32 * q + 4 : 32 * q + 12, :], tab_s32[0:2, 4 * q : 4 * q + 4, :])
+        for half in range(2):
+            rows = w1[0:N, half * N // 2 : (half + 1) * N // 2]
+            nc.sync.dma_start(first_raw[half][:], rows.rearrange("(p j) c -> p j c", j=4))
         for r in range(4):
             nc.sync.dma_start(w4s_raw[r:P:32, :], w4_s32[0, r:16:4, :])
         load_tab(W4_PASS)
@@ -232,14 +252,15 @@ def tile_list_clamped_actuator_commands_kernel(
 
         deal(w4_w[:].bitcast(U16), w4_raw[:].bitcast(U16))
         gather_words(0, 0, S)
-        cast_shared(0)
+        cast_first()
         gather(v_s[:], tab_s[:].bitcast(U8), offs_sb[:])
-        deal(w4_s[:], w4s_raw[:].bitcast(U8))
         quantise_w1(0, 0)
         for u in range(2):
             project(0, u, one_pass(0))
-        gather_words(W4_PASS, 0, S)
+        w4_s = reused([P, H], U8, "w4_s", "w1_bf00")
+        deal(w4_s[:], w4s_raw[:].bitcast(U8))
         for u in range(2):
+            gather_words(W4_PASS, N * u, N * (u + 1))
             project(0, u, one_pass(W4_PASS))
         cast_shared(1)
         gather(v2_s[:], tab2_s[:].bitcast(U8), offs2_sb[:])
@@ -253,51 +274,55 @@ def tile_list_clamped_actuator_commands_kernel(
         project(1, 0, one_pass(W4_PASS))
         quantise_w1(0, 1)
         h_rows[0, 0] = reused([P, 4, N], BF16, "h_rows00", "w1_raw01")
-        clip(0, 0, range(2))
+        clip(0, 0)
         project(1, 0, one_pass(0))
+        round_p(0, 1)
+        first_early = held([P, N // 2, 4], BF16, "first_early")
+        weave_into(nc.scalar.copy, first_early[:], h_rows[0, 0][:, :, 0 : N // 2])
         cast_vector(1)
-        clip(0, 0, range(2, 4))
+        h_rows[0, 1] = reused([P, 4, N], BF16, "h_rows01", "w1_raw11")
         quantise_w1(1, 1)
         project(1, 0, one_pass(1))
-        round_p(0, 1)
+        clip(0, 1)
 
-        v2_w[0] = shared.tile([P, S2], U32, name="v2_w0", align_bytes=64, offset=0)
-        h_bf[0, 0] = shared.tile([P, N, 4], BF16, name="h_bf00", align_bytes=64, offset=4 * S2)
-        weave(nc.scalar.copy, 0, 0, 0, SCALAR_STATES_FIRST)
+        for b in range(2):
+            v2_w[b] = shared.tile([P, S2], U32, name="v2_w%d" % b, align_bytes=64, offset=4 * S2 * b)
+            gather(v2_w[b][:], tab2_w[b][:].bitcast(U32), offs2_sb[:])
+        first_late = reused([P, N // 2, 4], BF16, "first_late", "p_rows013")
+        gpsimd_copy(first_late[:], h_rows[0, 0][:, :, N // 2 : N].rearrange("p t n -> p n t"))
         gpsimd_copy(
-            h_bf[0, 0][:, SCALAR_STATES_FIRST:N, :],
-            h_rows[0, 0][:, :, SCALAR_STATES_FIRST:N].rearrange("p t n -> p n t"),
+            h_bf[0, 1][:, SCALAR_STATES_SECOND:N, :],
+            h_rows[0, 1][:, :, SCALAR_STATES_SECOND:N].rearrange("p t n -> p n t"),
         )
         round_p(1, 0)
         early, late = (W4_PASS, 0, 1), (1, W4_PASS, 0)
         project(1, 1, [(t, a) for t in range(4) for a in (early if t < 2 else late)])
         round_p(1, 1)
-        for b in range(2):
-            gather(v2_w[b][:], tab2_w[b][:].bitcast(U32), offs2_sb[:])
-        clip(1, 0)
-        h_rows[0, 1] = reused([P, 4, N], BF16, "h_rows01", "tab2_w0")
-        clip(0, 1)
-        h_bf[0, 1] = reused([P, N, 4], BF16, "h_bf01", "p_rows103")
-        weave(nc.scalar.copy, 0, 1)
-        quantise_h(0, 0)
+        weave(nc.scalar.copy, 0, 1, 0, SCALAR_STATES_SECOND)
+        h_w[0, 0] = reused([P, N], U32, "h_w00", "tab2_w1")
+        quantise_first(first_early, 0)
+        clip(1, 0, range(2))
+        quantise_first(first_late, N // 2)
+        clip(1, 0, range(2, 4))
         weave(nc.vector.tensor_copy, 1, 0)
         clip(1, 1)
         quantise_h(1, 0)
         dot(0)
-        weave(nc.scalar.copy, 1, 1, 0, SCALAR_STATES_LAST)
-        weave(nc.vector.tensor_copy, 1, 1, SCALAR_STATES_LAST, N)
+        weave(nc.scalar.copy, 1, 1)
+        quantise_h(0, 1)
 
         floor = reused([P, 4], F32, "floor", "p_rows110")
         nc.vector.tensor_tensor(out=floor[:], in0=cmin_sb[:], in1=cmax_sb[:], op=ALU.min)
         for c in range(4):
             scale(0, c)
             clamp_and_store(nc.gpsimd, floor, 0, c)
-            if c < 2:
-                quantise_h(c, 1)
-            if c == 1:
+            if c == 2:
+                quantise_h(1, 1)
                 dot(1)
         scale(1, 0)
-        for c in range(1, 4):
+        clamp_and_store(nc.gpsimd, floor, 1, 0)
+        scale(1, 1)
+        for c in range(2, 4):
             scale(1, c)
             clamp_and_store(nc.vector, floor, 1, c - 1)
         clamp_and_store(nc.vector, floor, 1, 3)

@@ -20,6 +20,7 @@ FLOPS = 2 * K * H * S + 2 * H * S2 * S
 
 SCALAR_QUADS = (96, 80)
 SCALAR_STATES_SECOND = 384
+SCALAR_STATES_LAST = 256
 
 
 def tile_list_clamped_actuator_commands_kernel(
@@ -308,16 +309,17 @@ def tile_list_clamped_actuator_commands_kernel(
         clip(1, 1)
         quantise_h(1, 0)
         dot(0)
-        weave(nc.scalar.copy, 1, 1)
-        quantise_h(0, 1)
+        weave(nc.scalar.copy, 1, 1, 0, SCALAR_STATES_LAST)
+        weave(nc.vector.tensor_copy, 1, 1, SCALAR_STATES_LAST, N)
 
         floor = reused([P, 4], F32, "floor", "p_rows110")
         nc.vector.tensor_tensor(out=floor[:], in0=cmin_sb[:], in1=cmax_sb[:], op=ALU.min)
         for c in range(4):
             scale(0, c)
             clamp_and_store(nc.gpsimd, floor, 0, c)
-            if c == 2:
-                quantise_h(1, 1)
+            if c < 2:
+                quantise_h(c, 1)
+            if c == 1:
                 dot(1)
         scale(1, 0)
         clamp_and_store(nc.gpsimd, floor, 1, 0)

@@ -69,11 +69,16 @@ def tile_list_clamped_actuator_commands_kernel(
             rows = w1[N * a : N * (a + 1), N * b : N * (b + 1)]
             nc.sync.dma_start(w1_raw[a, b][:], rows.rearrange("(p j) c -> p j c", j=4))
 
-        def load_tab2_scales(quadrants):
-            for q in quadrants:
-                nc.sync.dma_start(tab2_s[32 * q + 8 : 32 * q + 16, :], tab2_s32[:, 4 * q : 4 * q + 4, :])
+        def load_first(half):
+            rows = w1[0:N, half * N // 2 : (half + 1) * N // 2]
+            nc.sync.dma_start(first_raw[half][:], rows.rearrange("(p j) c -> p j c", j=4))
+
+        def load_limits(b):
+            for tile, limit in ((lo_sb, lo), (hi_sb, hi)):
+                nc.sync.dma_start(tile[:, b, 0:4], limit[N * b : N * (b + 1)].rearrange("(p t) -> p t", t=4))
 
         w4_w = held([P, 2 * H], U8, "w4_w")
+        w4_s = held([P, H], U8, "w4_s")
         v_w = [held([P, S], U32, "v_w%d" % a) for a in range(3)]
         v_s = held([P, S], U8, "v_s")
         v2_w = {}
@@ -214,52 +219,48 @@ def tile_list_clamped_actuator_commands_kernel(
             )
             nc.sync.dma_start(out[P * c : P * (c + 1), N * u : N * (u + 1)], res[:])
 
+        nc.gpsimd.memset(w4s_raw[:], 0)
         nc.vector.memset(tab_s[:], 0)
-        nc.vector.memset(w4s_raw[:], 0)
         nc.vector.memset(tab2_s[:], 0)
         for q in range(2, 4):
             nc.gpsimd.dma_start(tab_s[32 * q + 4 : 32 * q + 12, :], tab_s32[0:2, 4 * q : 4 * q + 4, :])
-        for half in range(2):
-            words = slice(half * H // 4, (half + 1) * H // 4)
-            nc.sync.dma_start(w4_raw[:, words], w4_words[0].bitcast(I32)[:, words])
-        nc.sync.dma_start(offs_sb[:], offs)
-        nc.sync.dma_start(lo_sb[:, :, 0:4], lo.rearrange("(b p t) -> p b t", b=2, t=4))
-        nc.sync.dma_start(hi_sb[:, :, 0:4], hi.rearrange("(b p t) -> p b t", b=2, t=4))
-        nc.sync.dma_start(offs2_sb[:], offs2)
+        for q in range(4):
+            nc.gpsimd.dma_start(tab2_s[32 * q + 8 : 32 * q + 16, :], tab2_s32[:, 4 * q : 4 * q + 4, :])
+        nc.sync.dma_start(w4_raw[:], w4_words[0].bitcast(I32))
         load_tab(0, 0, T // 2)
+        nc.sync.dma_start(offs_sb[:], offs)
+        for r in range(4):
+            nc.sync.dma_start(w4s_raw[r:P:32, :], w4_s32[0, r:16:4, :])
         load_tab(0, T // 2, T)
+        load_first(0)
         for r in range(4):
             nc.sync.dma_start(tab_s[r:P:32, :], tab_s32[W4_PASS, r:16:4, :])
         for q in range(2):
             nc.sync.dma_start(tab_s[32 * q + 4 : 32 * q + 12, :], tab_s32[0:2, 4 * q : 4 * q + 4, :])
-        for half in range(2):
-            rows = w1[0:N, half * N // 2 : (half + 1) * N // 2]
-            nc.sync.dma_start(first_raw[half][:], rows.rearrange("(p j) c -> p j c", j=4))
-        for r in range(4):
-            nc.sync.dma_start(w4s_raw[r:P:32, :], w4_s32[0, r:16:4, :])
+        load_first(1)
         load_tab(W4_PASS)
-        load_tab2_scales(range(2))
+        nc.sync.dma_start(offs2_sb[:], offs2)
         load_w1(1, 0)
-        load_tab2_scales(range(2, 4))
         load_tab(1)
+        load_limits(0)
         load_w1(0, 1)
         load_w1(1, 1)
         load_tab2(0)
         load_tab2(1)
+        load_limits(1)
         with nc.allow_non_contiguous_dma(reason="one limit a partition"):
             nc.sync.dma_start(cmin_sb[:], cmin.rearrange("(c p) -> p c", p=P))
             nc.sync.dma_start(cmax_sb[:], cmax.rearrange("(c p) -> p c", p=P))
         nc.sync.dma_start(gain_sb[:], gain.partition_broadcast(P))
 
         deal(w4_w[:].bitcast(U16), w4_raw[:].bitcast(U16))
+        deal(w4_s[:], w4s_raw[:].bitcast(U8))
         gather_words(0, 0, S)
         cast_first()
         gather(v_s[:], tab_s[:].bitcast(U8), offs_sb[:])
         quantise_w1(0, 0)
         for u in range(2):
             project(0, u, one_pass(0))
-        w4_s = reused([P, H], U8, "w4_s", "w1_bf00")
-        deal(w4_s[:], w4s_raw[:].bitcast(U8))
         for u in range(2):
             gather_words(W4_PASS, N * u, N * (u + 1))
             project(0, u, one_pass(W4_PASS))

@@ -103,8 +103,8 @@ def tile_list_clamped_actuator_commands_kernel(
             split = SCALAR_QUADS[a]
             dst, raw = cast_views(a, 0, "m j t")
             nc.scalar.copy(out=dst[:, 0:split], in_=raw[:, 0:split])
-            dst, raw = cast_views(a, 0, "t m j")
-            gpsimd_copy(dst[:, :, split:P], raw[:, :, split:P])
+            dst, raw = cast_views(a, 0, "m t j")
+            gpsimd_copy(dst[:, split:P], raw[:, split:P])
 
         def cast_first():
             split = SCALAR_QUADS[0]
@@ -112,19 +112,21 @@ def tile_list_clamped_actuator_commands_kernel(
             raw = [tile[:].rearrange("p j (m t) -> p m j t", t=4) for tile in first_raw]
             nc.scalar.copy(out=dst[:, 0 : P // 2], in_=raw[0])
             nc.scalar.copy(out=dst[:, P // 2 : split], in_=raw[1][:, 0 : split - P // 2])
-            dst = w1_bf[0, 0][:].rearrange("p (t m j) -> p t m j", t=4, j=4)
-            raw = first_raw[1][:].rearrange("p j (m t) -> p t m j", t=4)
-            gpsimd_copy(dst[:, :, split:P], raw[:, :, split - P // 2 : P // 2])
+            dst = w1_bf[0, 0][:].rearrange("p (t m j) -> p m t j", t=4, j=4)
+            raw = first_raw[1][:].rearrange("p j (m t) -> p m t j", t=4)
+            gpsimd_copy(dst[:, split:P], raw[:, split - P // 2 : P // 2])
 
-        def cast_vector(a):
+        def cast_vector(a, t0=0, t1=4):
             dst, raw = cast_views(a, 1, "m j t")
-            nc.vector.tensor_copy(out=dst, in_=raw)
+            nc.vector.tensor_copy(out=dst[:, :, :, t0:t1], in_=raw[:, :, :, t0:t1])
 
         def gpsimd_copy(dst, src):
             nc.gpsimd.tensor_scalar(out=dst, in0=src, scalar1=1.0, scalar2=0.0, op0=ALU.mult, op1=ALU.add)
 
-        def quantise_w1(a, b):
-            nc.vector.quantize_mx(out=w1_w[a, b][:].bitcast(FP8X4), scales=w1_s[a, b][:], in_=w1_bf[a, b][:])
+        def quantise_w1(a, b, c0=0, c1=N):
+            nc.vector.quantize_mx(
+                out=w1_w[a, b][:, c0:c1].bitcast(FP8X4), scales=w1_s[a, b][:, c0:c1], in_=w1_bf[a, b][:, 4 * c0 : 4 * c1]
+            )
 
         def gather(dst, window, offsets):
             nc.vector.tensor_copy(out=dst, in_=window.indirect(offsets))
@@ -242,8 +244,8 @@ def tile_list_clamped_actuator_commands_kernel(
         nc.sync.dma_start(offs2_sb[:], offs2)
         load_w1(1, 0)
         load_tab(1)
-        load_limits(0)
         load_w1(0, 1)
+        load_limits(0)
         load_w1(1, 1)
         load_tab2(0)
         load_tab2(1)
@@ -272,18 +274,22 @@ def tile_list_clamped_actuator_commands_kernel(
             project(0, u, one_pass(1))
 
         round_p(0, 0)
-        cast_vector(0)
+        for half in range(2):
+            cast_vector(0, 2 * half, 2 * half + 2)
         project(1, 0, one_pass(W4_PASS))
-        quantise_w1(0, 1)
-        h_rows[0, 0] = reused([P, 4, N], BF16, "h_rows00", "w1_raw01")
+        for half in range(2):
+            quantise_w1(0, 1, half * N // 2, (half + 1) * N // 2)
+        h_rows[0, 0] = held([P, 4, N], BF16, "h_rows00")
         clip(0, 0)
         project(1, 0, one_pass(0))
         round_p(0, 1)
         first_early = held([P, N // 2, 4], BF16, "first_early")
         weave_into(nc.scalar.copy, first_early[:], h_rows[0, 0][:, :, 0 : N // 2])
-        cast_vector(1)
+        for half in range(2):
+            cast_vector(1, 2 * half, 2 * half + 2)
         h_rows[0, 1] = reused([P, 4, N], BF16, "h_rows01", "w1_raw11")
-        quantise_w1(1, 1)
+        for half in range(2):
+            quantise_w1(1, 1, half * N // 2, (half + 1) * N // 2)
         project(1, 0, one_pass(1))
         clip(0, 1)
 
@@ -302,10 +308,10 @@ def tile_list_clamped_actuator_commands_kernel(
         round_p(1, 1)
         weave(nc.scalar.copy, 0, 1, 0, SCALAR_STATES_SECOND)
         h_w[0, 0] = reused([P, N], U32, "h_w00", "tab2_w1")
-        quantise_first(first_early, 0)
         clip(1, 0, range(2))
-        quantise_first(first_late, N // 2)
+        quantise_first(first_early, 0)
         clip(1, 0, range(2, 4))
+        quantise_first(first_late, N // 2)
         weave(nc.vector.tensor_copy, 1, 0)
         clip(1, 1)
         quantise_h(1, 0)

@@ -18,7 +18,7 @@ N = 512
 W4_PASS = 2
 FLOPS = 2 * K * H * S + 2 * H * S2 * S
 
-SCALAR_QUADS = (96, 80)
+SCALAR_QUADS = (80, 80)
 SCALAR_STATES_SECOND = 384
 SCALAR_STATES_LAST = 256
 
@@ -47,8 +47,7 @@ def tile_list_clamped_actuator_commands_kernel(
         w4_raw = held([P, H // 2], I32, "w4_raw")
         w4s_raw = held([P, H // 4], I32, "w4s_raw")
         blocks = [(a, b) for a in range(2) for b in range(2)]
-        w1_raw = {key: held([P, 4, N], F32, "w1_raw%d%d" % key) for key in blocks[1:]}
-        first_raw = [held([P, 4, N // 2], F32, "first_raw%d" % half) for half in range(2)]
+        w1_raw = {key: held([P, 4, N], F32, "w1_raw%d%d" % key) for key in blocks}
         lo_sb = held([P, 2, 8], F32, "lo_sb")
         hi_sb = held([P, 2, 8], F32, "hi_sb")
         cmin_sb = held([P, 4], F32, "cmin_sb")
@@ -69,10 +68,6 @@ def tile_list_clamped_actuator_commands_kernel(
             rows = w1[N * a : N * (a + 1), N * b : N * (b + 1)]
             nc.sync.dma_start(w1_raw[a, b][:], rows.rearrange("(p j) c -> p j c", j=4))
 
-        def load_first(half):
-            rows = w1[0:N, half * N // 2 : (half + 1) * N // 2]
-            nc.sync.dma_start(first_raw[half][:], rows.rearrange("(p j) c -> p j c", j=4))
-
         def load_limits(b):
             for tile, limit in ((lo_sb, lo), (hi_sb, hi)):
                 nc.sync.dma_start(tile[:, b, 0:4], limit[N * b : N * (b + 1)].rearrange("(p t) -> p t", t=4))
@@ -80,7 +75,7 @@ def tile_list_clamped_actuator_commands_kernel(
         w4_w = held([P, 2 * H], U8, "w4_w")
         w4_s = held([P, H], U8, "w4_s")
         v_w = [held([P, S], U32, "v_w%d" % a) for a in range(3)]
-        v_s = held([P, S], U8, "v_s")
+        v_s = [held([P, N], U8, "v_s%d" % u) for u in range(2)]
         v2_w = {}
         v2_s = held([P, S2], U8, "v2_s")
         w1_bf = {key: held([P, 4 * N], BF16, "w1_bf%d%d" % key) for key in blocks[:3]}
@@ -88,8 +83,8 @@ def tile_list_clamped_actuator_commands_kernel(
         w1_w = {key: held([P, N], U32, "w1_w%d%d" % key) for key in blocks}
         w1_s = {key: held([P, N], U8, "w1_s%d%d" % key) for key in blocks}
 
-        def deal(dst, src):
-            nc.vector.tensor_copy(
+        def deal(copy, dst, src):
+            copy(
                 out=dst.rearrange("p (b t m) -> p b t m", b=2, t=4), in_=src.rearrange("p (b m t) -> p b t m", b=2, t=4)
             )
 
@@ -105,16 +100,6 @@ def tile_list_clamped_actuator_commands_kernel(
             nc.scalar.copy(out=dst[:, 0:split], in_=raw[:, 0:split])
             dst, raw = cast_views(a, 0, "m t j")
             gpsimd_copy(dst[:, split:P], raw[:, split:P])
-
-        def cast_first():
-            split = SCALAR_QUADS[0]
-            dst = w1_bf[0, 0][:].rearrange("p (t m j) -> p m j t", t=4, j=4)
-            raw = [tile[:].rearrange("p j (m t) -> p m j t", t=4) for tile in first_raw]
-            nc.scalar.copy(out=dst[:, 0 : P // 2], in_=raw[0])
-            nc.scalar.copy(out=dst[:, P // 2 : split], in_=raw[1][:, 0 : split - P // 2])
-            dst = w1_bf[0, 0][:].rearrange("p (t m j) -> p m t j", t=4, j=4)
-            raw = first_raw[1][:].rearrange("p j (m t) -> p m t j", t=4)
-            gpsimd_copy(dst[:, split:P], raw[:, split - P // 2 : P // 2])
 
         def cast_vector(a, t0=0, t1=4):
             dst, raw = cast_views(a, 1, "m j t")
@@ -147,11 +132,11 @@ def tile_list_clamped_actuator_commands_kernel(
                     c0 = N * b + P * t
                     lhs = w4_w[:, 2 * c0 : 2 * (c0 + P)].bitcast(FP4X4)
                     lhs_s = w4_s[:, c0 : c0 + P]
-                    rhs_s = v_s[:, cols]
+                    rhs_s = v_s[u][:]
                 else:
                     lhs = w1_w[a, b][:, P * t : P * (t + 1)].bitcast(FP8X4)
                     lhs_s = w1_s[a, b][:, P * t : P * (t + 1)]
-                    rhs_s = v_s[4 * a + 4 : P, cols]
+                    rhs_s = v_s[u][4 * a + 4 : P, :]
                 nc.tensor.matmul_mx(
                     out=acc[b, u, t][:], lhsT=lhs, lhsT_scale=lhs_s, rhs=v_w[a][:, cols].bitcast(FP8X4), rhs_scale=rhs_s,
                     start=(passes_done[b, u, t] == 1), stop=(passes_done[b, u, t] == 3),
@@ -224,23 +209,20 @@ def tile_list_clamped_actuator_commands_kernel(
         nc.gpsimd.memset(w4s_raw[:], 0)
         nc.vector.memset(tab_s[:], 0)
         nc.vector.memset(tab2_s[:], 0)
-        for q in range(2, 4):
+        for q in range(4):
             nc.gpsimd.dma_start(tab_s[32 * q + 4 : 32 * q + 12, :], tab_s32[0:2, 4 * q : 4 * q + 4, :])
         for q in range(4):
             nc.gpsimd.dma_start(tab2_s[32 * q + 8 : 32 * q + 16, :], tab2_s32[:, 4 * q : 4 * q + 4, :])
-        nc.sync.dma_start(w4_raw[:], w4_words[0].bitcast(I32))
         load_tab(0, 0, T // 2)
         nc.sync.dma_start(offs_sb[:], offs)
         for r in range(4):
             nc.sync.dma_start(w4s_raw[r:P:32, :], w4_s32[0, r:16:4, :])
         load_tab(0, T // 2, T)
-        load_first(0)
+        load_tab(W4_PASS)
         for r in range(4):
             nc.sync.dma_start(tab_s[r:P:32, :], tab_s32[W4_PASS, r:16:4, :])
-        for q in range(2):
-            nc.sync.dma_start(tab_s[32 * q + 4 : 32 * q + 12, :], tab_s32[0:2, 4 * q : 4 * q + 4, :])
-        load_first(1)
-        load_tab(W4_PASS)
+        nc.sync.dma_start(w4_raw[:], w4_words[0].bitcast(I32))
+        load_w1(0, 0)
         nc.sync.dma_start(offs2_sb[:], offs2)
         load_w1(1, 0)
         load_tab(1)
@@ -255,17 +237,17 @@ def tile_list_clamped_actuator_commands_kernel(
             nc.sync.dma_start(cmax_sb[:], cmax.rearrange("(c p) -> p c", p=P))
         nc.sync.dma_start(gain_sb[:], gain.partition_broadcast(P))
 
-        deal(w4_w[:].bitcast(U16), w4_raw[:].bitcast(U16))
-        deal(w4_s[:], w4s_raw[:].bitcast(U8))
+        deal(nc.vector.tensor_copy, w4_s[:], w4s_raw[:].bitcast(U8))
         gather_words(0, 0, S)
-        cast_first()
-        gather(v_s[:], tab_s[:].bitcast(U8), offs_sb[:])
+        deal(nc.scalar.copy, w4_w[:].bitcast(U16), w4_raw[:].bitcast(U16))
+        for u in range(2):
+            gather_words(W4_PASS, N * u, N * (u + 1))
+            gather(v_s[u][:], tab_s[:].bitcast(U8), offs_sb[:, N * u // 16 : N * (u + 1) // 16])
+            project(0, u, one_pass(W4_PASS))
+        cast_shared(0)
         quantise_w1(0, 0)
         for u in range(2):
             project(0, u, one_pass(0))
-        for u in range(2):
-            gather_words(W4_PASS, N * u, N * (u + 1))
-            project(0, u, one_pass(W4_PASS))
         cast_shared(1)
         gather(v2_s[:], tab2_s[:].bitcast(U8), offs2_sb[:])
         quantise_w1(1, 0)

@@ -18,7 +18,7 @@ N = 512
 W4_PASS = 2
 FLOPS = 2 * K * H * S + 2 * H * S2 * S
 
-SCALAR_QUADS = (80, 80)
+SCALAR_QUADS = 80
 SCALAR_STATES_SECOND = 384
 SCALAR_STATES_LAST = 256
 
@@ -30,6 +30,7 @@ def tile_list_clamped_actuator_commands_kernel(
     with ExitStack() as ctx:
         keep = ctx.enter_context(tc.tile_pool(name="keep", bufs=1))
         shared = ctx.enter_context(tc.tile_pool(name="shared", bufs=1))
+        early = ctx.enter_context(tc.tile_pool(name="early", bufs=1))
         psum = ctx.enter_context(tc.psum_pool(name="psum", bufs=8))
 
         def held(shape, dtype, name):
@@ -74,11 +75,11 @@ def tile_list_clamped_actuator_commands_kernel(
 
         w4_w = held([P, 2 * H], U8, "w4_w")
         w4_s = held([P, H], U8, "w4_s")
-        v_w = [held([P, S], U32, "v_w%d" % a) for a in range(3)]
+        v_w = [held([P, S], U32, "v_w%d" % a) for a in range(2)]
         v_s = [held([P, N], U8, "v_s%d" % u) for u in range(2)]
         v2_w = {}
-        v2_s = held([P, S2], U8, "v2_s")
-        w1_bf = {key: held([P, 4 * N], BF16, "w1_bf%d%d" % key) for key in blocks[:3]}
+        w1_bf = {(0, 0): early.tile([P, 4 * N], BF16, name="w1_bf00", align_bytes=64, offset=0)}
+        w1_bf[0, 1] = held([P, 4 * N], BF16, "w1_bf01")
         w1_bf[1, 1] = shared.tile([P, 4 * N], BF16, name="w1_bf11", align_bytes=64, offset=0)
         w1_w = {key: held([P, N], U32, "w1_w%d%d" % key) for key in blocks}
         w1_s = {key: held([P, N], U8, "w1_s%d%d" % key) for key in blocks}
@@ -95,7 +96,7 @@ def tile_list_clamped_actuator_commands_kernel(
             )
 
         def cast_shared(a):
-            split = SCALAR_QUADS[a]
+            split = SCALAR_QUADS
             dst, raw = cast_views(a, 0, "m j t")
             nc.scalar.copy(out=dst[:, 0:split], in_=raw[:, 0:split])
             dst, raw = cast_views(a, 0, "m t j")
@@ -132,13 +133,13 @@ def tile_list_clamped_actuator_commands_kernel(
                     c0 = N * b + P * t
                     lhs = w4_w[:, 2 * c0 : 2 * (c0 + P)].bitcast(FP4X4)
                     lhs_s = w4_s[:, c0 : c0 + P]
-                    rhs_s = v_s[u][:]
+                    rhs, rhs_s = w4_v[u][:], v_s[u][:]
                 else:
                     lhs = w1_w[a, b][:, P * t : P * (t + 1)].bitcast(FP8X4)
                     lhs_s = w1_s[a, b][:, P * t : P * (t + 1)]
-                    rhs_s = v_s[u][4 * a + 4 : P, :]
+                    rhs, rhs_s = v_w[a][:, cols], v_s[u][4 * a + 4 : P, :]
                 nc.tensor.matmul_mx(
-                    out=acc[b, u, t][:], lhsT=lhs, lhsT_scale=lhs_s, rhs=v_w[a][:, cols].bitcast(FP8X4), rhs_scale=rhs_s,
+                    out=acc[b, u, t][:], lhsT=lhs, lhsT_scale=lhs_s, rhs=rhs.bitcast(FP8X4), rhs_scale=rhs_s,
                     start=(passes_done[b, u, t] == 1), stop=(passes_done[b, u, t] == 3),
                 )
 
@@ -209,7 +210,7 @@ def tile_list_clamped_actuator_commands_kernel(
         nc.gpsimd.memset(w4s_raw[:], 0)
         nc.vector.memset(tab_s[:], 0)
         nc.vector.memset(tab2_s[:], 0)
-        for q in range(4):
+        for q in range(1, 4):
             nc.gpsimd.dma_start(tab_s[32 * q + 4 : 32 * q + 12, :], tab_s32[0:2, 4 * q : 4 * q + 4, :])
         for q in range(4):
             nc.gpsimd.dma_start(tab2_s[32 * q + 8 : 32 * q + 16, :], tab2_s32[:, 4 * q : 4 * q + 4, :])
@@ -221,6 +222,7 @@ def tile_list_clamped_actuator_commands_kernel(
         load_tab(W4_PASS)
         for r in range(4):
             nc.sync.dma_start(tab_s[r:P:32, :], tab_s32[W4_PASS, r:16:4, :])
+        nc.sync.dma_start(tab_s[4:12, :], tab_s32[0:2, 0:4, :])
         nc.sync.dma_start(w4_raw[:], w4_words[0].bitcast(I32))
         load_w1(0, 0)
         nc.sync.dma_start(offs2_sb[:], offs2)
@@ -240,17 +242,25 @@ def tile_list_clamped_actuator_commands_kernel(
         deal(nc.vector.tensor_copy, w4_s[:], w4s_raw[:].bitcast(U8))
         gather_words(0, 0, S)
         deal(nc.scalar.copy, w4_w[:].bitcast(U16), w4_raw[:].bitcast(U16))
+        w4_v = [held([P, N], U32, "w4_v0"), reused([P, N], U32, "w4_v1", "w4_raw")]
         for u in range(2):
-            gather_words(W4_PASS, N * u, N * (u + 1))
-            gather(v_s[u][:], tab_s[:].bitcast(U8), offs_sb[:, N * u // 16 : N * (u + 1) // 16])
+            entries = offs_sb[:, N * u // 16 : N * (u + 1) // 16]
+            gather(w4_v[u][:], tab_w[W4_PASS][:].bitcast(U32), entries)
+            gather(v_s[u][:], tab_s[:].bitcast(U8), entries)
             project(0, u, one_pass(W4_PASS))
         cast_shared(0)
         quantise_w1(0, 0)
         for u in range(2):
             project(0, u, one_pass(0))
-        cast_shared(1)
+        three = held([P, 3 * N], BF16, "three")
+        last = early.tile([P, N], BF16, name="last", align_bytes=64, offset=0)
+        v2_s = early.tile([P, S2], U8, name="v2_s", align_bytes=64, offset=2 * N)
+        raw = w1_raw[1, 0][:].rearrange("p j (m t) -> p m j t", t=4)
+        nc.scalar.copy(out=three[:].rearrange("p (t m j) -> p m j t", t=3, j=4), in_=raw[:, :, :, 0:3])
+        gpsimd_copy(last[:].rearrange("p (m j) -> p m j", j=4), raw[:, :, :, 3])
         gather(v2_s[:], tab2_s[:].bitcast(U8), offs2_sb[:])
-        quantise_w1(1, 0)
+        for tile, cols in ((last, slice(3 * P, N)), (three, slice(0, 3 * P))):
+            nc.vector.quantize_mx(out=w1_w[1, 0][:, cols].bitcast(FP8X4), scales=w1_s[1, 0][:, cols], in_=tile[:])
         for u in range(2):
             gather_words(1, N * u, N * (u + 1))
             project(0, u, one_pass(1))
@@ -285,8 +295,8 @@ def tile_list_clamped_actuator_commands_kernel(
             h_rows[0, 1][:, :, SCALAR_STATES_SECOND:N].rearrange("p t n -> p n t"),
         )
         round_p(1, 0)
-        early, late = (W4_PASS, 0, 1), (1, W4_PASS, 0)
-        project(1, 1, [(t, a) for t in range(4) for a in (early if t < 2 else late)])
+        soon, late = (W4_PASS, 0, 1), (1, W4_PASS, 0)
+        project(1, 1, [(t, a) for t in range(4) for a in (soon if t < 2 else late)])
         round_p(1, 1)
         weave(nc.scalar.copy, 0, 1, 0, SCALAR_STATES_SECOND)
         h_w[0, 0] = reused([P, N], U32, "h_w00", "tab2_w1")

from contextlib import ExitStack

import concourse.mybir as mybir

F32 = mybir.dt.float32
BF16 = mybir.dt.bfloat16
I32 = mybir.dt.int32
U32 = mybir.dt.uint32
U16 = mybir.dt.uint16
U8 = mybir.dt.uint8
FP8X4 = mybir.dt.float8_e4m3fn_x4
FP4X4 = mybir.dt.float4_e2m1fn_x4
ALU = mybir.AluOpType

P = 128
K, H, T, S, T2, S2 = 1536, 1024, 2048, 1024, 1024, 512
N = 512
W4_PASS = 2
FLOPS = 2 * K * H * S + 2 * H * S2 * S

SCALAR_QUADS = 80
SCALAR_STATES_SECOND = 384
SCALAR_STATES_LAST = 256


def tile_list_clamped_actuator_commands_kernel(
    tc, tab_words, tab_scales, offs, tab2_words, tab2_scales, offs2, w1, w4_words, w4_scales, lo, hi, gain, cmin, cmax, out
):
    nc = tc.nc
    with ExitStack() as ctx:
        keep = ctx.enter_context(tc.tile_pool(name="keep", bufs=1))
        shared = ctx.enter_context(tc.tile_pool(name="shared", bufs=1))
        early = ctx.enter_context(tc.tile_pool(name="early", bufs=1))
        psum = ctx.enter_context(tc.psum_pool(name="psum", bufs=8))

        def held(shape, dtype, name):
            return keep.tile(shape, dtype, name=name, align_bytes=64)

        def reused(shape, dtype, name, after):
            return keep.tile(shape, dtype, name=name, tag=after, align_bytes=64)

        offs_sb = keep.tile([P, S // 16], U16, name="offs_sb")
        offs2_sb = keep.tile([P, S2 // 16], U16, name="offs2_sb")
        tab_w = [held([P, T], I32, "tab_w%d" % a) for a in range(3)]
        tab_s = held([P, T // 4], I32, "tab_s")
        tab2_w = [held([P, T2], I32, "tab2_w%d" % b) for b in range(2)]
        tab2_s = held([P, T2 // 4], I32, "tab2_s")
        w4_raw = held([P, H // 2], I32, "w4_raw")
        w4s_raw = held([P, H // 4], I32, "w4s_raw")
        blocks = [(a, b) for a in range(2) for b in range(2)]
        w1_raw = {key: held([P, 4, N], F32, "w1_raw%d%d" % key) for key in blocks}
        lo_sb = held([P, 2, 8], F32, "lo_sb")
        hi_sb = held([P, 2, 8], F32, "hi_sb")
        cmin_sb = held([P, 4], F32, "cmin_sb")
        cmax_sb = held([P, 4], F32, "cmax_sb")
        gain_sb = held([P, S], F32, "gain_sb")

        tab_s32 = tab_scales.bitcast(I32)
        tab2_s32 = tab2_scales.bitcast(I32)
        w4_s32 = w4_scales.bitcast(I32)

        def load_tab(a, t0=0, t1=T):
            nc.sync.dma_start(tab_w[a][:, t0:t1], tab_words[a].rearrange("p t i -> p (t i)").bitcast(I32)[:, t0:t1])

        def load_tab2(b):
            nc.sync.dma_start(tab2_w[b][:], tab2_words[b].rearrange("p t i -> p (t i)").bitcast(I32))

        def load_w1(a, b):
            rows = w1[N * a : N * (a + 1), N * b : N * (b + 1)]
            nc.sync.dma_start(w1_raw[a, b][:], rows.rearrange("(p j) c -> p j c", j=4))

        def load_limits(b):
            for tile, limit in ((lo_sb, lo), (hi_sb, hi)):
                nc.sync.dma_start(tile[:, b, 0:4], limit[N * b : N * (b + 1)].rearrange("(p t) -> p t", t=4))

        w4_w = held([P, 2 * H], U8, "w4_w")
        w4_s = held([P, H], U8, "w4_s")
        v_w = [held([P, S], U32, "v_w%d" % a) for a in range(2)]
        v_s = [held([P, N], U8, "v_s%d" % u) for u in range(2)]
        v2_w = {}
        w1_bf = {(0, 0): early.tile([P, 4 * N], BF16, name="w1_bf00", align_bytes=64, offset=0)}
        w1_bf[0, 1] = held([P, 4 * N], BF16, "w1_bf01")
        w1_bf[1, 1] = shared.tile([P, 4 * N], BF16, name="w1_bf11", align_bytes=64, offset=0)
        w1_w = {key: held([P, N], U32, "w1_w%d%d" % key) for key in blocks}
        w1_s = {key: held([P, N], U8, "w1_s%d%d" % key) for key in blocks}

        def deal(copy, dst, src):
            copy(
                out=dst.rearrange("p (b t m) -> p b t m", b=2, t=4), in_=src.rearrange("p (b m t) -> p b t m", b=2, t=4)
            )

        def cast_views(a, b, order):
            return (
                w1_bf[a, b][:].rearrange("p (t m j) -> p " + order, t=4, j=4),
                w1_raw[a, b][:].rearrange("p j (m t) -> p " + order, t=4),
            )

        def cast_shared(a):
            split = SCALAR_QUADS
            dst, raw = cast_views(a, 0, "m j t")
            nc.scalar.copy(out=dst[:, 0:split], in_=raw[:, 0:split])
            dst, raw = cast_views(a, 0, "m t j")
            gpsimd_copy(dst[:, split:P], raw[:, split:P])

        def cast_vector(a, t0=0, t1=4):
            dst, raw = cast_views(a, 1, "m j t")
            nc.vector.tensor_copy(out=dst[:, :, :, t0:t1], in_=raw[:, :, :, t0:t1])

        def gpsimd_copy(dst, src):
            nc.gpsimd.tensor_scalar(out=dst, in0=src, scalar1=1.0, scalar2=0.0, op0=ALU.mult, op1=ALU.add)

        def quantise_w1(a, b, c0=0, c1=N):
            nc.vector.quantize_mx(
                out=w1_w[a, b][:, c0:c1].bitcast(FP8X4), scales=w1_s[a, b][:, c0:c1], in_=w1_bf[a, b][:, 4 * c0 : 4 * c1]
            )

        def gather(dst, window, offsets):
            nc.vector.tensor_copy(out=dst, in_=window.indirect(offsets))

        def gather_words(a, j0, j1):
            gather(v_w[a][:, j0:j1], tab_w[a][:].bitcast(U32), offs_sb[:, j0 // 16 : j1 // 16])

        acc = {}
        passes_done = {}

        def project(b, u, steps):
            cols = slice(N * u, N * (u + 1))
            for t, a in steps:
                passes_done[b, u, t] = passes_done.get((b, u, t), 0) + 1
                if passes_done[b, u, t] == 1:
                    acc[b, u, t] = psum.tile([P, N], F32, name="bank")
                if a == W4_PASS:
                    c0 = N * b + P * t
                    lhs = w4_w[:, 2 * c0 : 2 * (c0 + P)].bitcast(FP4X4)
                    lhs_s = w4_s[:, c0 : c0 + P]
                    rhs, rhs_s = w4_v[u][:], v_s[u][:]
                else:
                    lhs = w1_w[a, b][:, P * t : P * (t + 1)].bitcast(FP8X4)
                    lhs_s = w1_s[a, b][:, P * t : P * (t + 1)]
                    rhs, rhs_s = v_w[a][:, cols], v_s[u][4 * a + 4 : P, :]
                nc.tensor.matmul_mx(
                    out=acc[b, u, t][:], lhsT=lhs, lhsT_scale=lhs_s, rhs=rhs.bitcast(FP8X4), rhs_scale=rhs_s,
                    start=(passes_done[b, u, t] == 1), stop=(passes_done[b, u, t] == 3),
                )

        def one_pass(a):
            return [(t, a) for t in range(4)]

        groups = [(b, u) for b in range(2) for u in range(2)]
        p_rows = {g: [held([P, N], BF16, "p_rows%d%d%d" % (g + (t,))) for t in range(4)] for g in groups}
        h_rows = {(1, u): held([P, 4, N], BF16, "h_rows1%d" % u) for u in range(2)}
        h_bf = {g: held([P, N, 4], BF16, "h_bf%d%d" % g) for g in groups[1:]}
        h_w = {g: held([P, N], U32, "h_w%d%d" % g) for g in groups[1:]}
        h_s = {g: held([P, N], U8, "h_s%d%d" % g) for g in groups}

        def round_p(b, u):
            for t in range(4):
                nc.scalar.copy(out=p_rows[b, u][t][:], in_=acc[b, u, t][:])

        def clip(b, u, banks=range(4)):
            for t in banks:
                nc.vector.tensor_scalar(
                    out=h_rows[b, u][:, t, :], in0=p_rows[b, u][t][:], scalar1=lo_sb[:, b, t : t + 1],
                    scalar2=hi_sb[:, b, t : t + 1], op0=ALU.max, op1=ALU.min,
                )

        def weave_into(copy, dst, rows):
            copy(out=dst.rearrange("p (c i) t -> p c t i", i=4), in_=rows.rearrange("p t (c i) -> p c t i", i=4))

        def weave(copy, b, u, n0=0, n1=N):
            weave_into(copy, h_bf[b, u][:, n0:n1, :], h_rows[b, u][:, :, n0:n1])

        def quantise_first(woven, n0):
            cols = slice(n0, n0 + N // 2)
            nc.vector.quantize_mx(
                out=h_w[0, 0][:, cols].bitcast(FP8X4), scales=h_s[0, 0][:, cols], in_=woven[:].rearrange("p n t -> p (n t)")
            )

        def quantise_h(b, u):
            nc.vector.quantize_mx(
                out=h_w[b, u][:].bitcast(FP8X4), scales=h_s[b, u][:], in_=h_bf[b, u][:].rearrange("p n t -> p (n t)")
            )

        y = {}
        scaled = {}

        def dot(u):
            for b in range(2):
                for c in range(4):
                    if b == 0:
                        y[u, c] = psum.tile([P, N], F32, name="bank")
                    nc.tensor.matmul_mx(
                        out=y[u, c][:], lhsT=v2_w[b][:, P * c : P * (c + 1)].bitcast(FP8X4),
                        lhsT_scale=v2_s[4 * b + 8 : P, P * c : P * (c + 1)],
                        rhs=h_w[b, u][:].bitcast(FP8X4), rhs_scale=h_s[b, u][:], start=(b == 0), stop=(b == 1),
                    )

        def scale(u, c):
            scaled[u, c] = held([P, N], F32, "scaled%d%d" % (u, c))
            nc.vector.tensor_tensor(out=scaled[u, c][:], in0=y[u, c][:], in1=gain_sb[:, N * u : N * (u + 1)], op=ALU.mult)

        def clamp_and_store(engine, floor, u, c):
            res = held([P, N], F32, "res%d%d" % (u, c))
            engine.tensor_scalar(
                out=res[:], in0=scaled[u, c][:], scalar1=cmax_sb[:, c : c + 1], scalar2=floor[:, c : c + 1],
                op0=ALU.min, op1=ALU.max,
            )
            nc.sync.dma_start(out[P * c : P * (c + 1), N * u : N * (u + 1)], res[:])

        nc.gpsimd.memset(w4s_raw[:], 0)
        nc.vector.memset(tab_s[:], 0)
        nc.vector.memset(tab2_s[:], 0)
        for q in range(1, 4):
            nc.gpsimd.dma_start(tab_s[32 * q + 4 : 32 * q + 12, :], tab_s32[0:2, 4 * q : 4 * q + 4, :])
        for q in range(4):
            nc.gpsimd.dma_start(tab2_s[32 * q + 8 : 32 * q + 16, :], tab2_s32[:, 4 * q : 4 * q + 4, :])
        load_tab(0, 0, T // 2)
        nc.sync.dma_start(offs_sb[:], offs)
        for r in range(4):
            nc.sync.dma_start(w4s_raw[r:P:32, :], w4_s32[0, r:16:4, :])
        load_tab(0, T // 2, T)
        load_tab(W4_PASS)
        for r in range(4):
            nc.sync.dma_start(tab_s[r:P:32, :], tab_s32[W4_PASS, r:16:4, :])
        nc.sync.dma_start(tab_s[4:12, :], tab_s32[0:2, 0:4, :])
        nc.sync.dma_start(w4_raw[:], w4_words[0].bitcast(I32))
        load_w1(0, 0)
        nc.sync.dma_start(offs2_sb[:], offs2)
        load_w1(1, 0)
        load_tab(1)
        load_w1(0, 1)
        load_limits(0)
        load_w1(1, 1)
        load_tab2(0)
        load_tab2(1)
        load_limits(1)
        with nc.allow_non_contiguous_dma(reason="one limit a partition"):
            nc.sync.dma_start(cmin_sb[:], cmin.rearrange("(c p) -> p c", p=P))
            nc.sync.dma_start(cmax_sb[:], cmax.rearrange("(c p) -> p c", p=P))
        nc.sync.dma_start(gain_sb[:], gain.partition_broadcast(P))

        deal(nc.vector.tensor_copy, w4_s[:], w4s_raw[:].bitcast(U8))
        gather_words(0, 0, S)
        deal(nc.scalar.copy, w4_w[:].bitcast(U16), w4_raw[:].bitcast(U16))
        w4_v = [held([P, N], U32, "w4_v0"), reused([P, N], U32, "w4_v1", "w4_raw")]
        for u in range(2):
            entries = offs_sb[:, N * u // 16 : N * (u + 1) // 16]
            gather(w4_v[u][:], tab_w[W4_PASS][:].bitcast(U32), entries)
            gather(v_s[u][:], tab_s[:].bitcast(U8), entries)
            project(0, u, one_pass(W4_PASS))
        cast_shared(0)
        quantise_w1(0, 0)
        for u in range(2):
            project(0, u, one_pass(0))
        three = held([P, 3 * N], BF16, "three")
        last = early.tile([P, N], BF16, name="last", align_bytes=64, offset=0)
        v2_s = early.tile([P, S2], U8, name="v2_s", align_bytes=64, offset=2 * N)
        raw = w1_raw[1, 0][:].rearrange("p j (m t) -> p m j t", t=4)
        nc.scalar.copy(out=three[:].rearrange("p (t m j) -> p m j t", t=3, j=4), in_=raw[:, :, :, 0:3])
        gpsimd_copy(last[:].rearrange("p (m j) -> p m j", j=4), raw[:, :, :, 3])
        gather(v2_s[:], tab2_s[:].bitcast(U8), offs2_sb[:])
        for tile, cols in ((last, slice(3 * P, N)), (three, slice(0, 3 * P))):
            nc.vector.quantize_mx(out=w1_w[1, 0][:, cols].bitcast(FP8X4), scales=w1_s[1, 0][:, cols], in_=tile[:])
        for u in range(2):
            gather_words(1, N * u, N * (u + 1))
            project(0, u, one_pass(1))

        round_p(0, 0)
        for half in range(2):
            cast_vector(0, 2 * half, 2 * half + 2)
        project(1, 0, one_pass(W4_PASS))
        for half in range(2):
            quantise_w1(0, 1, half * N // 2, (half + 1) * N // 2)
        h_rows[0, 0] = held([P, 4, N], BF16, "h_rows00")
        clip(0, 0)
        project(1, 0, one_pass(0))
        round_p(0, 1)
        first_early = held([P, N // 2, 4], BF16, "first_early")
        weave_into(nc.scalar.copy, first_early[:], h_rows[0, 0][:, :, 0 : N // 2])
        for half in range(2):
            cast_vector(1, 2 * half, 2 * half + 2)
        h_rows[0, 1] = reused([P, 4, N], BF16, "h_rows01", "w1_raw11")
        for half in range(2):
            quantise_w1(1, 1, half * N // 2, (half + 1) * N // 2)
        project(1, 0, one_pass(1))
        clip(0, 1)

        for b in range(2):
            v2_w[b] = shared.tile([P, S2], U32, name="v2_w%d" % b, align_bytes=64, offset=4 * S2 * b)
            gather(v2_w[b][:], tab2_w[b][:].bitcast(U32), offs2_sb[:])
        first_late = reused([P, N // 2, 4], BF16, "first_late", "p_rows013")
        gpsimd_copy(first_late[:], h_rows[0, 0][:, :, N // 2 : N].rearrange("p t n -> p n t"))
        gpsimd_copy(
            h_bf[0, 1][:, SCALAR_STATES_SECOND:N, :],
            h_rows[0, 1][:, :, SCALAR_STATES_SECOND:N].rearrange("p t n -> p n t"),
        )
        round_p(1, 0)
        soon, late = (W4_PASS, 0, 1), (1, W4_PASS, 0)
        project(1, 1, [(t, a) for t in range(4) for a in (soon if t < 2 else late)])
        round_p(1, 1)
        weave(nc.scalar.copy, 0, 1, 0, SCALAR_STATES_SECOND)
        h_w[0, 0] = reused([P, N], U32, "h_w00", "tab2_w1")
        clip(1, 0, range(2))
        quantise_first(first_early, 0)
        clip(1, 0, range(2, 4))
        quantise_first(first_late, N // 2)
        weave(nc.vector.tensor_copy, 1, 0)
        clip(1, 1)
        quantise_h(1, 0)
        dot(0)
        weave(nc.scalar.copy, 1, 1, 0, SCALAR_STATES_LAST)
        weave(nc.vector.tensor_copy, 1, 1, SCALAR_STATES_LAST, N)

        floor = reused([P, 4], F32, "floor", "p_rows110")
        nc.vector.tensor_tensor(out=floor[:], in0=cmin_sb[:], in1=cmax_sb[:], op=ALU.min)
        for c in range(4):
            scale(0, c)
            clamp_and_store(nc.gpsimd, floor, 0, c)
            if c < 2:
                quantise_h(c, 1)
            if c == 1:
                dot(1)
        scale(1, 0)
        clamp_and_store(nc.gpsimd, floor, 1, 0)
        scale(1, 1)
        for c in range(2, 4):
            scale(1, c)
            clamp_and_store(nc.vector, floor, 1, c - 1)
        clamp_and_store(nc.vector, floor, 1, 3)
